import numpy as np
import ml_dtypes


def mxq(x, axis, fmt="e4m3"):
    dtype, down = {"e4m3": (ml_dtypes.float8_e4m3fn, 7), "e5m2": (ml_dtypes.float8_e5m2, 14)}[fmt]
    v = np.moveaxis(np.asarray(x, np.float32).astype(ml_dtypes.bfloat16).astype(np.float64), axis, -1)
    blocks = v.reshape(v.shape[:-1] + (-1, 32))
    amax = np.abs(blocks).max(-1, keepdims=True)
    byte = np.maximum(np.where(amax > 0, np.frexp(amax)[1] - 1 + 127, 0) - down, 1)
    scale = np.exp2(byte - 127.0)
    codes = (blocks / scale).astype(np.float32).astype(dtype).astype(np.float64)
    return np.moveaxis((codes * scale).reshape(v.shape), -1, axis)


WIDE = False


def mx_kscale(k):
    if not WIDE:
        return np.ones(k)
    levels = np.array([10, -10, 5, -5, 0])
    if k % 512:
        return np.exp2(np.random.permutation(np.resize(levels, k // 32))).repeat(32)
    a = np.empty((k // 512, 16))
    for p in range(k // 512):
        a[p, :8] = np.random.permutation(np.resize(levels, 8))
        for g in range(8):
            far = levels[np.abs(levels - a[p, g]) >= 10]
            a[p, g + 8] = far[np.random.randint(len(far))]
    return np.exp2(a.ravel()).repeat(32)


BF16 = ml_dtypes.bfloat16


def bf(x):
    return np.asarray(x, np.float32).astype(BF16)


def f64(x):
    return np.asarray(x).astype(np.float64)


E2M1 = np.array([0.0, 0.5, 1.0, 1.5, 2.0, 3.0, 4.0, 6.0, -0.0, -0.5, -1.0, -1.5, -2.0, -3.0, -4.0, -6.0])


def pack_weight(w, fmt):
    k, n = w.shape
    w = f64(bf(w)).reshape(k // 32, 32, n)
    amax = np.abs(w).max(1)
    if fmt == "e4m3":
        byte = np.frexp(amax)[1] - 1 + 127 - 7
    else:
        mant, ex = np.frexp(amax / 6.0)
        byte = np.where(mant > 0.5, ex, ex - 1) + 127
    byte = np.clip(np.where(amax > 0, byte, 1), 1, 254)
    scaled = (w * np.exp2(127.0 - byte)[:, None, :]).reshape(k, n).astype(np.float32)
    by_word = np.ascontiguousarray(scaled.reshape(k // 512, 128, 4, n).transpose(0, 1, 3, 2))
    if fmt == "e4m3":
        words = by_word.astype(ml_dtypes.float8_e4m3fn).view(np.uint8)
    else:
        c = by_word.astype(ml_dtypes.float4_e2m1fn).view(np.uint8) & 0xF
        words = c[..., 0::2] | (c[..., 1::2] << 4)
    return np.ascontiguousarray(words), np.ascontiguousarray(byte.astype(np.uint8).reshape(k // 512, 16, n))


def unpack_weight(words, scales, fmt):
    g, p, n, _ = words.shape
    if fmt == "e4m3":
        vals = np.ascontiguousarray(words).view(ml_dtypes.float8_e4m3fn).astype(np.float64)
    else:
        nib = np.empty((g, p, n, 4), np.uint8)
        nib[..., 0::2] = words & 0xF
        nib[..., 1::2] = words >> 4
        vals = E2M1[nib]
    vals = vals * np.repeat(np.exp2(scales.astype(np.float64) - 127.0), 8, axis=1)[..., None]
    return vals.transpose(0, 1, 3, 2).reshape(g * 512, n)

def planes(Y):
    n, m = Y.shape
    b = f64(bf(Y)).reshape(n // 32, 32, m)
    amax = np.abs(b).max(1)
    byte = np.clip(np.where(amax > 0, np.frexp(amax)[1] - 1 + 127 - 7, 1), 1, 254)
    codes = (b * np.exp2(127.0 - byte)[:, None, :]).reshape(n, m).astype(np.float32).astype(ml_dtypes.float8_e4m3fn).view(np.uint8)
    words = codes.reshape(n // 512, 128, 4, m).transpose(0, 1, 3, 2)
    return np.ascontiguousarray(words), np.ascontiguousarray(byte.astype(np.uint8).reshape(n // 512, 16, m))


N, D, F, E = 1024, 512, 512, 4


def setup_inputs():
    s, t = mx_kscale(D), mx_kscale(N)
    x = np.random.standard_normal((N, D)) * s
    a = np.random.standard_normal((E, N, N)) * (1.5 / np.sqrt(N)) / t
    w = np.random.standard_normal((E, D, F)) * (1.5 / np.sqrt(D)) / s[:, None]
    c = (1.0 + 0.1 * np.random.standard_normal(N)) * t
    b = np.random.standard_normal((E, F)) * 0.5
    wg = np.random.standard_normal((D, E)) * (2.0 / np.sqrt(D)) / s[:, None]
    w0 = np.random.standard_normal((D, F)) * (0.7 / np.sqrt(D)) / s[:, None]
    w0_words, w0_scales = pack_weight(w0, "e4m3")
    return {"x": bf(x), "a": bf(a), "w": bf(w), "c": bf(c), "b": bf(b), "wg": bf(wg), "w0_words": w0_words, "w0_scales": w0_scales}


def gate_weights(x, wg):
    z = np.sum(x[:, None, :] * wg.T[None, :, :], axis=-1)
    u = np.exp(z - z.max(axis=-1, keepdims=True))
    return u / u.sum(axis=-1, keepdims=True)


def relation_experts(xq, a, w, c, b):
    p = c[None, :, None] * (xq @ mxq(w, 1, "e4m3"))
    agg = mxq(a, 2, "e4m3") @ mxq(p, 1, "e4m3")
    return np.maximum(agg + b[:, None, :], 0.0)


def core(x, a, w, c, b, wg, w0_words, w0_scales):
    x = f64(x)
    g = gate_weights(x, f64(wg))
    xq = mxq(x, 1, "e4m3")
    h = relation_experts(xq, f64(a), f64(w), f64(c), f64(b))
    r = xq @ unpack_weight(w0_words, w0_scales, "e4m3")
    return r + np.sum(g.T[:, :, None] * h, axis=0)


def reference(x, a, w, c, b, wg, w0_words, w0_scales):
    R_out = core(x, a, w, c, b, wg, w0_words, w0_scales)
    words, scales = planes(R_out)
    return R_out, words, scales

@@ -1,0 +1,418 @@
+from contextlib import ExitStack
+
+import concourse.mybir as mybir
+from concourse.masks import make_identity
+
+F32 = mybir.dt.float32
+BF16 = mybir.dt.bfloat16
+U32 = mybir.dt.uint32
+I32 = mybir.dt.int32
+U8 = mybir.dt.uint8
+FP8X4 = mybir.dt.float8_e4m3fn_x4
+ACT = mybir.ActivationFunctionType
+ALU = mybir.AluOpType
+AX = mybir.AxisListType
+
+N, D, F, E = 1024, 512, 512, 4
+P = 128
+FLOPS = 2 * (E * N * D * F + E * N * N * F + N * D * F)
+STEPS = 16
+FORM = "anan"
+TURNED = [e for e in range(E) if FORM[e] == "a"]
+PLAIN = [e for e in range(E) if FORM[e] == "n"]
+
+
+def tile_relationalgraphmixtureofexperts_x2_kernel(tc, x, a, w, c, b, wg, w0_words, w0_scales, out_0, out_1, out_2):
+    nc = tc.nc
+    with ExitStack() as ctx:
+        keep = ctx.enter_context(tc.tile_pool(name="keep", bufs=1))
+        work = ctx.enter_context(tc.tile_pool(name="work", bufs=3))
+        psum = ctx.enter_context(tc.psum_pool(name="psum", bufs=2))
+
+        ident = keep.tile([P, P], F32, name="ident", align_bytes=64)
+        make_identity(nc, ident[:])
+        ident_bf = keep.tile([P, P], BF16, name="ident_bf", align_bytes=64)
+        make_identity(nc, ident_bf[:])
+        b_rows = keep.tile([P, F], BF16, name="b_rows", align_bytes=64)
+        nc.gpsimd.memset(b_rows[:], 0.0)
+        g_parts = keep.tile([P, 8, P], BF16, name="g_parts", align_bytes=64)
+        nc.gpsimd.memset(g_parts[:], 0.0)
+        w0_sc = keep.tile([P, F], U8, name="w0_sc", align_bytes=64)
+        nc.gpsimd.memset(w0_sc[:].bitcast(I32), 0)
+
+        w0_codes = keep.tile([P, 4 * F], U8, name="w0_codes", align_bytes=64)
+        c_bf = keep.tile([P, 2, 4], BF16, name="c_bf", align_bytes=64)
+        wg_sb = keep.tile([P, 4, E], BF16, name="wg_sb", align_bytes=64)
+        x_raw, w_raw, a_raw = {}, {}, {}
+        b_bc, nb = {}, {}
+
+        def load_x(g):
+            x_raw[g] = work.tile([P, 4, D], BF16, name="x_raw", tag="raw", bufs=12, align_bytes=64)
+            nc.sync.dma_start(out=x_raw[g][:], in_=x[512 * g : 512 * g + 512, :].rearrange("(p t) k -> p t k", t=4))
+
+        def load_w(e):
+            w_raw[e] = work.tile([P, 4, F], BF16, name="w_raw", tag="raw", bufs=12, align_bytes=64)
+            nc.sync.dma_start(out=w_raw[e][:], in_=w[e].rearrange("(p j) f -> p j f", j=4))
+
+        def load_a(s):
+            e, g, h = s // 4, (s // 2) % 2, s % 2
+            src = a[e, 512 * g : 512 * g + 512, :].rearrange("(p t) m -> p t m", t=4)
+            a_raw[s] = work.tile([P, 2, N], BF16, name="a_raw", tag="raw", bufs=12, align_bytes=64)
+            nc.sync.dma_start(out=a_raw[s][:], in_=src[:, 2 * h : 2 * h + 2, :])
+
+        load_x(0)
+        load_w(0)
+        nc.gpsimd.dma_start(out=wg_sb[:], in_=wg.rearrange("(p t) e -> p t e", t=4))
+        nc.gpsimd.dma_start(out=c_bf[:], in_=c.rearrange("(h p t) -> p h t", p=P, t=4))
+        for j in range(3):
+            nc.gpsimd.dma_start(out=b_rows[4 * j : 4 * j + 4, :], in_=b)
+        load_x(1)
+        load_a(0)
+        load_a(1)
+        load_w(1)
+        load_a(2)
+        load_a(3)
+        nc.sync.dma_start(out=w0_codes[:].bitcast(I32), in_=w0_words[0].rearrange("p n t -> p (n t)").bitcast(I32))
+        for q in range(4):
+            nc.sync.dma_start(out=w0_sc[32 * q : 32 * q + 4, :].bitcast(I32), in_=w0_scales[0, 4 * q : 4 * q + 4, :].bitcast(I32))
+        for e in PLAIN:
+            b_bc[e] = keep.tile([P, F], BF16, name="b_bc%d" % e, align_bytes=64)
+            nc.sync.dma_start(out=b_bc[e][:], in_=b[e].partition_broadcast(P))
+        load_w(2)
+        load_w(3)
+        for s in range(4, STEPS):
+            load_a(s)
+
+        c_f = keep.tile([P, 8], F32, name="c_f", align_bytes=64)
+        nc.vector.tensor_copy(out=c_f[:], in_=c_bf[:].rearrange("p h t -> p (h t)"))
+
+        x_t = work.tile([P, 4096], BF16, name="x_t", tag="a_t", bufs=2, align_bytes=64)
+        x_codes = keep.tile([P, 8 * P], U32, name="x_codes", align_bytes=64)
+        x_sc = keep.tile([P, 8 * P], U8, name="x_sc", align_bytes=64)
+
+        def turn_x(g):
+            words = x_raw[g][:].rearrange("p t k -> p (t k)").bitcast(F32)
+            for half in range(2):
+                bank = psum.tile([P, 512], F32, name="tp", tag="tp", bufs=3)
+                for tt in range(2):
+                    for u in range(2):
+                        lo = 256 * (2 * half + tt) + u
+                        nc.tensor.transpose(bank[:, 128 * (2 * tt + u) : 128 * (2 * tt + u) + 128], words[:, lo : lo + 256 - u : 2], ident[:])
+                c0 = 2048 * g + 1024 * half
+                nc.scalar.copy(
+                    out=x_t[:, c0 : c0 + 1024].bitcast(F32).rearrange("p (t n u) -> p t n u", t=2, u=2),
+                    in_=bank[:].rearrange("p (t u n) -> p t n u", t=2, u=2),
+                )
+
+        def quant_x(g):
+            cols = slice(512 * g, 512 * g + 512)
+            nc.vector.quantize_mx(out=x_codes[:, cols].bitcast(FP8X4), scales=x_sc[:, cols], in_=x_t[:, 2048 * g : 2048 * g + 2048])
+
+        w_codes, w_sc, w_grp = {}, {}, {}
+
+        def group_w(e):
+            w_grp[e] = work.tile([P, F, 4], BF16, name="w_grp", tag="grp", bufs=5, align_bytes=64)
+            nc.vector.tensor_copy(out=w_grp[e][:], in_=w_raw[e][:].rearrange("p j f -> p f j"))
+
+        def quant_w(e):
+            w_codes[e] = keep.tile([P, F], U32, name="w_codes%d" % e, align_bytes=64)
+            w_sc[e] = keep.tile([P, F], U8, name="w_sc%d" % e, align_bytes=64)
+            nc.vector.quantize_mx(out=w_codes[e][:].bitcast(FP8X4), scales=w_sc[e][:], in_=w_grp[e][:].rearrange("p f j -> p (f j)"))
+
+        a_t, a_codes, a_sc = {}, {}, {}
+
+        def turn_a(s):
+            v, half = s // 2, s % 2
+            words = a_raw[s][:].rearrange("p t m -> p (t m)").bitcast(F32)
+            if half == 0:
+                a_t[v] = work.tile([P, 4096], BF16, name="a_t", tag="a_t", bufs=2, align_bytes=64)
+            dst = a_t[v][:].bitcast(F32).rearrange("p (h t n u) -> p h t n u", h=2, t=4, u=2)
+            for tt in range(2):
+                bank = psum.tile([P, 512], F32, name="tp", tag="tp", bufs=3)
+                for h in range(2):
+                    for u in range(2):
+                        lo = 512 * tt + 256 * h + u
+                        nc.tensor.transpose(bank[:, 128 * (2 * h + u) : 128 * (2 * h + u) + 128], words[:, lo : lo + 256 - u : 2], ident[:])
+                nc.scalar.copy(out=dst[:, :, 2 * half + tt], in_=bank[:].rearrange("p (h u n) -> p h n u", h=2, u=2))
+
+        def quant_a(v, h):
+            if h == 0:
+                a_codes[v] = work.tile([P, 1024], U32, name="a_codes", tag="a_codes", bufs=3, align_bytes=64)
+                a_sc[v] = work.tile([P, 1024], U8, name="a_sc", tag="a_sc", bufs=3, align_bytes=64)
+            cols = slice(512 * h, 512 * h + 512)
+            nc.vector.quantize_mx(out=a_codes[v][:, cols].bitcast(FP8X4), scales=a_sc[v][:, cols], in_=a_t[v][:, 2048 * h : 2048 * h + 2048])
+
+        p_raw, p_grp, p_codes, p_sc = {}, {}, {}, {}
+
+        def mx(out, lhs, rhs, start, stop):
+            nc.tensor.matmul_mx(
+                out=out, lhsT=lhs[0].bitcast(FP8X4), lhsT_scale=lhs[1], rhs=rhs[0].bitcast(FP8X4), rhs_scale=rhs[1], start=start, stop=stop
+            )
+
+        def x_tile(i):
+            return x_codes[:, 128 * i : 128 * i + 128], x_sc[:, 128 * i : 128 * i + 128]
+
+        def project(e, i, on_vector):
+            h, t = i // 4, i % 4
+            if t == 0:
+                p_raw[e, h] = work.tile([P, 4, F], BF16, name="p_raw", tag="p_raw", bufs=3, align_bytes=64)
+            bank = psum.tile([P, 512], F32, name="pp", tag="pp", bufs=2)
+            mx(bank[:], x_tile(i), (w_codes[e][:], w_sc[e][:]), True, True)
+            dst = p_raw[e, h][:, t, :]
+            if on_vector:
+                nc.vector.tensor_scalar(out=dst, in0=bank[:], scalar1=c_f[:, i : i + 1], scalar2=None, op0=ALU.mult)
+            else:
+                nc.scalar.activation(out=dst, in_=bank[:], func=ACT.Copy, scale=c_f[:, i : i + 1])
+
+        def group_p(e, h, part):
+            if (e, h) not in p_grp:
+                p_grp[e, h] = work.tile([P, F, 4], BF16, name="p_grp", tag="grp", bufs=5, align_bytes=64)
+            f0 = 256 * part
+            dst = p_grp[e, h][:, f0 : f0 + 256, :]
+            src = p_raw[e, h][:, :, f0 : f0 + 256].rearrange("p t f -> p f t")
+            if part == 0:
+                nc.vector.tensor_copy(out=dst, in_=src)
+            else:
+                nc.scalar.copy(out=dst, in_=src)
+
+        def quant_p(e, h):
+            p_codes[e, h] = work.tile([P, F], U32, name="p_codes", tag="p_codes", bufs=5, align_bytes=64)
+            p_sc[e, h] = work.tile([P, F], U8, name="p_sc", tag="p_sc", bufs=5, align_bytes=64)
+            nc.vector.quantize_mx(out=p_codes[e, h][:].bitcast(FP8X4), scales=p_sc[e, h][:], in_=p_grp[e, h][:].rearrange("p f t -> p (f t)"))
+
+        agg, proj0 = {}, {}
+
+        def aggregate(s):
+            v, e, g = s // 2, s // 4, (s // 2) % 2
+            for q in (2 * (s % 2), 2 * (s % 2) + 1):
+                agg[v, q] = psum.tile([P, 512], F32, name="ag", tag="ag", bufs=3)
+                for h in range(2):
+                    if FORM[e] == "a":
+                        fs = slice(128 * q, 128 * q + 128)
+                        lhs = (p_codes[e, h][:, fs], p_sc[e, h][:, fs])
+                        rhs = (a_codes[v][:, 512 * h : 512 * h + 512], a_sc[v][:, 512 * h : 512 * h + 512])
+                    else:
+                        ns = slice(512 * h + 128 * q, 512 * h + 128 * q + 128)
+                        lhs = (a_codes[v][:, ns], a_sc[v][:, ns])
+                        rhs = (p_codes[e, h][:], p_sc[e, h][:])
+                    mx(agg[v, q][:], lhs, rhs, h == 0, h == 1)
+                if e == PLAIN[0]:
+                    proj0[v, q] = psum.tile([P, 512], F32, name="ag", tag="ag", bufs=3)
+                    mx(proj0[v, q][:], x_tile(4 * g + q), (w0_codes[:], w0_sc[:]), True, True)
+
+        acc = keep.tile([P, 8, F], F32, name="acc", align_bytes=64)
+        u_t, turned, res, sums = {}, {}, {}, {}
+
+        def clamp(v, q):
+            u_t[v, q] = work.tile([P, F], F32, name="u_t", tag="u_t", bufs=4, align_bytes=64)
+            nc.vector.tensor_tensor(out=u_t[v, q][:], in0=agg[v, q][:], in1=nb[v // 2][:], op=ALU.max)
+
+        def result(i):
+            if i % 4 == 0:
+                res[i // 4] = work.tile([P, 4, F], F32, name="res", tag="big", bufs=5, align_bytes=64)
+            return res[i // 4][:, i % 4, :]
+
+        def weigh(v, q):
+            e, i = v // 2, 4 * (v % 2) + q
+            other = proj0[v, q][:] if e == PLAIN[0] else acc[:, i, :]
+            dst = result(i) if e == E - 1 else acc[:, i, :]
+            nc.vector.scalar_tensor_tensor(out=dst, in0=u_t[v, q][:], scalar=gate[:, i, e : e + 1], in1=other, op0=ALU.mult, op1=ALU.add)
+
+        def clamp_weigh(v, q):
+            e, g = v // 2, v % 2
+            if q == 0:
+                turned[v] = work.tile([P, 4, F], F32, name="turned", tag="big", bufs=5, align_bytes=64)
+            nc.vector.scalar_tensor_tensor(
+                out=turned[v][:, q, :], in0=agg[v, q][:], scalar=nb_col[:, q, e : e + 1], in1=g_rows[e][:, 512 * g : 512 * g + 512], op0=ALU.max, op1=ALU.mult
+            )
+
+        def turn_back(i):
+            g, t = i // 4, i % 4
+            sums[i] = psum.tile([P, 512], F32, name="ag", tag="ag", bufs=3)
+            nc.tensor.matmul(out=sums[i][:], lhsT=g_t[:, i, :], rhs=b_rows[:], start=True, stop=False)
+            for e in TURNED:
+                for q in range(4):
+                    nc.tensor.matmul(
+                        out=sums[i][:, 128 * q : 128 * q + 128],
+                        lhsT=turned[2 * e + g][:, q, 128 * t : 128 * t + 128],
+                        rhs=ident[:],
+                        is_transpose=True,
+                        start=False,
+                        stop=(e == TURNED[-1] and q == 3),
+                    )
+
+        def add_turned(i):
+            dst = acc[:, i, :] if TURNED[-1] < E - 1 else result(i)
+            nc.vector.tensor_tensor(out=dst, in0=sums[i][:], in1=acc[:, i, :], op=ALU.add)
+
+        def store(g, half):
+            nc.sync.dma_start(
+                out=out_0[512 * g : 512 * g + 512, :].rearrange("(p t) m -> p t m", t=4)[:, 2 * half : 2 * half + 2, :],
+                in_=res[g][:, 2 * half : 2 * half + 2, :],
+            )
+
+        def finish(g):
+            grp = work.tile([P, F, 4], BF16, name="o_grp", tag="grp", bufs=5, align_bytes=64)
+            codes = work.tile([P, F], U32, name="o_codes", tag="p_codes", bufs=5, align_bytes=64)
+            scs = work.tile([P, F], U8, name="o_sc", tag="p_sc", bufs=5, align_bytes=64)
+            for part in range(2):
+                f0 = 256 * part
+                dst = grp[:, f0 : f0 + 256, :]
+                src = res[g][:, :, f0 : f0 + 256].rearrange("p t f -> p f t")
+                if part == 0:
+                    nc.vector.tensor_copy(out=dst, in_=src)
+                else:
+                    nc.scalar.copy(out=dst, in_=src)
+            for part in range(2):
+                f0 = 256 * part
+                nc.vector.quantize_mx(
+                    out=codes[:, f0 : f0 + 256].bitcast(FP8X4), scales=scs[:, f0 : f0 + 256], in_=grp[:, f0 : f0 + 256, :].rearrange("p f t -> p (f t)")
+                )
+            nc.sync.dma_start(out=out_1[g].rearrange("p m t -> p (m t)").bitcast(I32), in_=codes[:].bitcast(I32))
+            for q in range(4):
+                nc.sync.dma_start(out=out_2[g, 4 * q : 4 * q + 4, :].bitcast(I32), in_=scs[32 * q : 32 * q + 4, :].bitcast(I32))
+
+        turn_x(0)
+        group_w(0)
+        quant_w(0)
+        quant_x(0)
+        turn_x(1)
+        zps = psum.tile([P, 512], F32, name="ag", tag="ag", bufs=3)
+
+        def gate_logits(g):
+            for i in range(4 * g, 4 * g + 4):
+                xs = x_t[:, 512 * i : 512 * i + 512].rearrange("p (n j) -> p n j", j=4)
+                for j in range(4):
+                    nc.tensor.matmul(out=zps[:, 4 * i : 4 * i + 4], lhsT=xs[:, :, j], rhs=wg_sb[:, j, :], start=(j == 0), stop=(j == 3))
+
+        nb_col = keep.tile([P, 4, E], F32, name="nb_col", align_bytes=64)
+        nb_bank = psum.tile([P, 4, P], BF16, name="tp", tag="tp", bufs=3)
+        for q in range(4):
+            nc.tensor.transpose(nb_bank[:, q, :], b_rows[:, 128 * q : 128 * q + 128], ident_bf[:])
+        nc.scalar.activation(out=nb_col[:], in_=nb_bank[:, :, 0:E], func=ACT.Copy, scale=-1.0)
+
+        gate_logits(0)
+        quant_x(1)
+        gate_logits(1)
+        for i in range(4):
+            project(0, i, i % 2 == 1)
+        z = zps[:, 0:32].rearrange("p (i e) -> p i e", e=E)
+        zmax = keep.tile([P, 8], F32, name="zmax", align_bytes=64)
+        nc.vector.reduce_max(out=zmax[:], in_=z, axis=AX.X)
+        zs = keep.tile([P, 8, E], F32, name="zs", align_bytes=64)
+        nc.vector.tensor_tensor(out=zs[:], in0=z, in1=zmax[:].unsqueeze(2).to_broadcast([P, 8, E]), op=ALU.subtract)
+        ez = keep.tile([P, 8, E], F32, name="ez", align_bytes=64)
+        nc.scalar.activation(out=ez[:], in_=zs[:], func=ACT.Exp)
+        turn_a(0)
+        group_p(0, 0, 0)
+        group_p(0, 0, 1)
+        zsum = keep.tile([P, 8], F32, name="zsum", align_bytes=64)
+        nc.vector.reduce_sum(out=zsum[:], in_=ez[:], axis=AX.X)
+        for i in range(4, 8):
+            project(0, i, i % 2 == 1)
+        zrec = keep.tile([P, 8], F32, name="zrec", align_bytes=64)
+        nc.vector.reciprocal(out=zrec[:], in_=zsum[:])
+        turn_a(1)
+        gate = keep.tile([P, 8, E], F32, name="gate", align_bytes=64)
+        nc.vector.tensor_tensor(out=gate[:], in0=ez[:], in1=zrec[:].unsqueeze(2).to_broadcast([P, 8, E]), op=ALU.mult)
+        quant_p(0, 0)
+        g_rows = {}
+        for e in TURNED:
+            g_rows[e] = keep.tile([P, N], F32, name="g_rows%d" % e, align_bytes=64)
+
+        def spread_gate(e, g):
+            bank = psum.tile([P, 512], F32, name="tp", tag="tp", bufs=3)
+            for t in range(4):
+                nc.tensor.transpose(bank[:, 128 * t : 128 * t + 128], gate[:, 4 * g + t, e : e + 1].to_broadcast([P, P]), ident[:])
+            nc.scalar.copy(out=g_rows[e][:, 512 * g : 512 * g + 512], in_=bank[:])
+
+        spread_gate(0, 0)
+        group_p(0, 1, 0)
+        group_p(0, 1, 1)
+        quant_a(0, 0)
+        quant_a(0, 1)
+        quant_p(0, 1)
+        for e in PLAIN:
+            nb[e] = keep.tile([P, F], BF16, name="nb%d" % e, align_bytes=64)
+            nc.vector.tensor_scalar(out=nb[e][:], in0=b_bc[e][:], scalar1=-1.0, scalar2=None, op0=ALU.mult)
+        group_w(1)
+        quant_w(1)
+        project(1, 0, False)
+        project(1, 1, False)
+        turn_a(2)
+
+        g_t = keep.tile([P, 8, P], BF16, name="g_t", align_bytes=64)
+
+        def split_gate():
+            r1 = keep.tile([P, 8, E], F32, name="g_r1", align_bytes=64)
+            r2 = keep.tile([P, 8, E], F32, name="g_r2", align_bytes=64)
+            nc.vector.tensor_copy(out=g_parts[:, :, 0:4], in_=gate[:])
+            nc.vector.tensor_tensor(out=r1[:], in0=gate[:], in1=g_parts[:, :, 0:4], op=ALU.subtract)
+            nc.vector.tensor_copy(out=g_parts[:, :, 4:8], in_=r1[:])
+            nc.vector.tensor_tensor(out=r2[:], in0=r1[:], in1=g_parts[:, :, 4:8], op=ALU.subtract)
+            nc.vector.tensor_copy(out=g_parts[:, :, 8:12], in_=r2[:])
+
+        def turn_gate():
+            bank = psum.tile([P, 8, P], BF16, name="tp", tag="tp", bufs=3)
+            for i in range(8):
+                nc.tensor.transpose(bank[:, i, :], g_parts[:, i, :], ident_bf[:])
+            nc.scalar.copy(out=g_t[:], in_=bank[:])
+
+        spread_at = {1: [(0, 1)], 2: [(e, 0) for e in TURNED[1:]], 3: [(e, 1) for e in TURNED[1:]]}
+        back_at = {}
+        for g in range(2):
+            for half in range(2):
+                back_at[4 * TURNED[-1] + 2 * g + 2 + half] = [4 * g + 2 * half, 4 * g + 2 * half + 1]
+        for s in range(STEPS + 2):
+            v, e, j = s // 2, s // 4, s % 4
+            if s < STEPS:
+                aggregate(s)
+                k, pe = (s + 1) % 4, (s + 1) // 4 + 1
+                if pe < E:
+                    project(pe, 2 * k, False)
+                    project(pe, 2 * k + 1, False)
+            for i in back_at.get(s, []):
+                turn_back(i)
+            for ee, g in spread_at.get(s, []):
+                spread_gate(ee, g)
+            if s + 3 < STEPS:
+                turn_a(s + 3)
+            if s == 4:
+                split_gate()
+                turn_gate()
+            if s >= STEPS:
+                for i in back_at.get(s, []):
+                    add_turned(i)
+                continue
+            if j == 3 and e + 1 < E:
+                group_p(e + 1, 1, 0)
+                group_p(e + 1, 1, 1)
+            q0, q1 = 2 * (s % 2), 2 * (s % 2) + 1
+            first = clamp if FORM[e] == "n" else clamp_weigh
+            first(v, q0)
+            if s % 2 == 1 and v + 1 < 8:
+                quant_a(v + 1, 0)
+            first(v, q1)
+            if s % 2 == 1 and v + 1 < 8:
+                quant_a(v + 1, 1)
+            if j == 3 and e + 1 < E:
+                quant_p(e + 1, 1)
+            if j == 2 and e + 1 < E:
+                quant_p(e + 1, 0)
+            if FORM[e] == "n":
+                weigh(v, q0)
+            if j == 0 and e + 2 < E:
+                group_w(e + 2)
+            if j == 1 and e + 1 < E:
+                group_p(e + 1, 0, 0)
+                group_p(e + 1, 0, 1)
+            if j == 1 and e + 2 < E:
+                quant_w(e + 2)
+            if FORM[e] == "n":
+                weigh(v, q1)
+            for i in back_at.get(s, []):
+                add_turned(i)
+            if e == 3 and FORM[3] == "n":
+                store(j // 2, j % 2)
+                if j % 2 == 1:
+                    finish(j // 2)

@@ -17,9 +17,10 @@ N, D, F, E = 1024, 512, 512, 4
 P = 128
 FLOPS = 2 * (E * N * D * F + E * N * N * F + N * D * F)
 STEPS = 16
-FORM = "anan"
+FORM = "nnnn"
 TURNED = [e for e in range(E) if FORM[e] == "a"]
 PLAIN = [e for e in range(E) if FORM[e] == "n"]
+VC = 0
 
 
 def tile_relationalgraphmixtureofexperts_x2_kernel(tc, x, a, w, c, b, wg, w0_words, w0_scales, out_0, out_1, out_2):
@@ -29,16 +30,19 @@ def tile_relationalgraphmixtureofexperts_x2_kernel(tc, x, a, w, c, b, wg, w0_wor
         work = ctx.enter_context(tc.tile_pool(name="work", bufs=3))
         psum = ctx.enter_context(tc.psum_pool(name="psum", bufs=2))
 
+
+        zeros = keep.tile([P, F], BF16, name="zeros", align_bytes=64)
+        nc.vector.memset(zeros[:], 0.0)
         ident = keep.tile([P, P], F32, name="ident", align_bytes=64)
         make_identity(nc, ident[:])
-        ident_bf = keep.tile([P, P], BF16, name="ident_bf", align_bytes=64)
-        make_identity(nc, ident_bf[:])
         b_rows = keep.tile([P, F], BF16, name="b_rows", align_bytes=64)
         nc.gpsimd.memset(b_rows[:], 0.0)
-        g_parts = keep.tile([P, 8, P], BF16, name="g_parts", align_bytes=64)
-        nc.gpsimd.memset(g_parts[:], 0.0)
         w0_sc = keep.tile([P, F], U8, name="w0_sc", align_bytes=64)
         nc.gpsimd.memset(w0_sc[:].bitcast(I32), 0)
+        ident_bf = keep.tile([P, P], BF16, name="ident_bf", align_bytes=64)
+        make_identity(nc, ident_bf[:])
+        g_parts = keep.tile([P, 8, P], BF16, name="g_parts", align_bytes=64)
+        nc.gpsimd.memset(g_parts[:], 0.0)
 
         w0_codes = keep.tile([P, 4 * F], U8, name="w0_codes", align_bytes=64)
         c_bf = keep.tile([P, 2, 4], BF16, name="c_bf", align_bytes=64)
@@ -62,47 +66,55 @@ def tile_relationalgraphmixtureofexperts_x2_kernel(tc, x, a, w, c, b, wg, w0_wor
 
         load_x(0)
         load_w(0)
-        nc.gpsimd.dma_start(out=wg_sb[:], in_=wg.rearrange("(p t) e -> p t e", t=4))
-        nc.gpsimd.dma_start(out=c_bf[:], in_=c.rearrange("(h p t) -> p h t", p=P, t=4))
-        for j in range(3):
-            nc.gpsimd.dma_start(out=b_rows[4 * j : 4 * j + 4, :], in_=b)
+        nc.sync.dma_start(out=c_bf[:], in_=c.rearrange("(h p t) -> p h t", p=P, t=4))
+        nc.sync.dma_start(out=wg_sb[:], in_=wg.rearrange("(p t) e -> p t e", t=4))
         load_x(1)
         load_a(0)
-        load_a(1)
         load_w(1)
-        load_a(2)
-        load_a(3)
+        load_a(1)
+        for e in PLAIN:
+            b_bc[e] = keep.tile([P, F], BF16, name="b_bc%d" % e, align_bytes=64)
+        nc.sync.dma_start(out=b_bc[0][:], in_=b[0].partition_broadcast(P))
         nc.sync.dma_start(out=w0_codes[:].bitcast(I32), in_=w0_words[0].rearrange("p n t -> p (n t)").bitcast(I32))
         for q in range(4):
             nc.sync.dma_start(out=w0_sc[32 * q : 32 * q + 4, :].bitcast(I32), in_=w0_scales[0, 4 * q : 4 * q + 4, :].bitcast(I32))
-        for e in PLAIN:
-            b_bc[e] = keep.tile([P, F], BF16, name="b_bc%d" % e, align_bytes=64)
-            nc.sync.dma_start(out=b_bc[e][:], in_=b[e].partition_broadcast(P))
+        load_a(2)
+        load_a(3)
+        for j in range(3):
+            nc.sync.dma_start(out=b_rows[4 * j : 4 * j + 4, :], in_=b)
         load_w(2)
+        for s in range(4, 8):
+            load_a(s)
+        for e in PLAIN[1:]:
+            nc.sync.dma_start(out=b_bc[e][:], in_=b[e].partition_broadcast(P))
         load_w(3)
-        for s in range(4, STEPS):
+        for s in range(8, STEPS):
             load_a(s)
 
-        c_f = keep.tile([P, 8], F32, name="c_f", align_bytes=64)
-        nc.vector.tensor_copy(out=c_f[:], in_=c_bf[:].rearrange("p h t -> p (h t)"))
-
-        x_t = work.tile([P, 4096], BF16, name="x_t", tag="a_t", bufs=2, align_bytes=64)
+        x_t = work.tile([P, 4096], BF16, name="x_t", tag="a_t", bufs=3, align_bytes=64)
         x_codes = keep.tile([P, 8 * P], U32, name="x_codes", align_bytes=64)
         x_sc = keep.tile([P, 8 * P], U8, name="x_sc", align_bytes=64)
 
-        def turn_x(g):
+        x_bank = {}
+
+        def turn_x(g, hold=False):
             words = x_raw[g][:].rearrange("p t k -> p (t k)").bitcast(F32)
             for half in range(2):
-                bank = psum.tile([P, 512], F32, name="tp", tag="tp", bufs=3)
+                bank = psum.tile([P, 512], F32, name="tp", tag="tp", bufs=2)
+                x_bank[g, half] = bank
                 for tt in range(2):
                     for u in range(2):
                         lo = 256 * (2 * half + tt) + u
                         nc.tensor.transpose(bank[:, 128 * (2 * tt + u) : 128 * (2 * tt + u) + 128], words[:, lo : lo + 256 - u : 2], ident[:])
-                c0 = 2048 * g + 1024 * half
-                nc.scalar.copy(
-                    out=x_t[:, c0 : c0 + 1024].bitcast(F32).rearrange("p (t n u) -> p t n u", t=2, u=2),
-                    in_=bank[:].rearrange("p (t u n) -> p t n u", t=2, u=2),
-                )
+                if half == 0 or not hold:
+                    turn_x_copy(g, half, nc.scalar.copy)
+
+        def turn_x_copy(g, half, copy):
+            c0 = 2048 * g + 1024 * half
+            copy(
+                out=x_t[:, c0 : c0 + 1024].bitcast(F32).rearrange("p (t n u) -> p t n u", t=2, u=2),
+                in_=x_bank[g, half][:].rearrange("p (t u n) -> p t n u", t=2, u=2),
+            )
 
         def quant_x(g):
             cols = slice(512 * g, 512 * g + 512)
@@ -112,7 +124,7 @@ def tile_relationalgraphmixtureofexperts_x2_kernel(tc, x, a, w, c, b, wg, w0_wor
 
         def group_w(e):
             w_grp[e] = work.tile([P, F, 4], BF16, name="w_grp", tag="grp", bufs=5, align_bytes=64)
-            nc.vector.tensor_copy(out=w_grp[e][:], in_=w_raw[e][:].rearrange("p j f -> p f j"))
+            nc.vector.tensor_copy(out=w_grp[e][:].rearrange("p (f i) j -> p f j i", i=4), in_=w_raw[e][:].rearrange("p j (f i) -> p f j i", i=4))
 
         def quant_w(e):
             w_codes[e] = keep.tile([P, F], U32, name="w_codes%d" % e, align_bytes=64)
@@ -121,19 +133,18 @@ def tile_relationalgraphmixtureofexperts_x2_kernel(tc, x, a, w, c, b, wg, w0_wor
 
         a_t, a_codes, a_sc = {}, {}, {}
 
-        def turn_a(s):
+        def turn_a(s, tt):
             v, half = s // 2, s % 2
             words = a_raw[s][:].rearrange("p t m -> p (t m)").bitcast(F32)
-            if half == 0:
-                a_t[v] = work.tile([P, 4096], BF16, name="a_t", tag="a_t", bufs=2, align_bytes=64)
+            if half == 0 and tt == 0:
+                a_t[v] = work.tile([P, 4096], BF16, name="a_t", tag="a_t", bufs=3, align_bytes=64)
             dst = a_t[v][:].bitcast(F32).rearrange("p (h t n u) -> p h t n u", h=2, t=4, u=2)
-            for tt in range(2):
-                bank = psum.tile([P, 512], F32, name="tp", tag="tp", bufs=3)
-                for h in range(2):
-                    for u in range(2):
-                        lo = 512 * tt + 256 * h + u
-                        nc.tensor.transpose(bank[:, 128 * (2 * h + u) : 128 * (2 * h + u) + 128], words[:, lo : lo + 256 - u : 2], ident[:])
-                nc.scalar.copy(out=dst[:, :, 2 * half + tt], in_=bank[:].rearrange("p (h u n) -> p h n u", h=2, u=2))
+            bank = psum.tile([P, 512], F32, name="tp", tag="tp", bufs=2)
+            for h in range(2):
+                for u in range(2):
+                    lo = 512 * tt + 256 * h + u
+                    nc.tensor.transpose(bank[:, 128 * (2 * h + u) : 128 * (2 * h + u) + 128], words[:, lo : lo + 256 - u : 2], ident[:])
+            nc.scalar.copy(out=dst[:, :, 2 * half + tt], in_=bank[:].rearrange("p (h u n) -> p h n u", h=2, u=2))
 
         def quant_a(v, h):
             if h == 0:
@@ -152,28 +163,34 @@ def tile_relationalgraphmixtureofexperts_x2_kernel(tc, x, a, w, c, b, wg, w0_wor
         def x_tile(i):
             return x_codes[:, 128 * i : 128 * i + 128], x_sc[:, 128 * i : 128 * i + 128]
 
-        def project(e, i, on_vector):
+        banks = {}
+
+        def project(e, i, tag="pp", bufs=2):
+            banks[e, i] = psum.tile([P, 512], F32, name=tag, tag=tag, bufs=bufs)
+            mx(banks[e, i][:], x_tile(i), (w_codes[e][:], w_sc[e][:]), True, True)
+
+        def scale_p(e, i, on_vector=False):
             h, t = i // 4, i % 4
             if t == 0:
                 p_raw[e, h] = work.tile([P, 4, F], BF16, name="p_raw", tag="p_raw", bufs=3, align_bytes=64)
-            bank = psum.tile([P, 512], F32, name="pp", tag="pp", bufs=2)
-            mx(bank[:], x_tile(i), (w_codes[e][:], w_sc[e][:]), True, True)
             dst = p_raw[e, h][:, t, :]
             if on_vector:
-                nc.vector.tensor_scalar(out=dst, in0=bank[:], scalar1=c_f[:, i : i + 1], scalar2=None, op0=ALU.mult)
+                nc.vector.tensor_scalar(out=dst, in0=banks[e, i][:], scalar1=c_f[:, i : i + 1], scalar2=None, op0=ALU.mult)
             else:
-                nc.scalar.activation(out=dst, in_=bank[:], func=ACT.Copy, scale=c_f[:, i : i + 1])
+                nc.scalar.activation(out=dst, in_=banks[e, i][:], func=ACT.Copy, scale=c_f[:, i : i + 1])
 
-        def group_p(e, h, part):
+        def group_p(e, h, vc=VC):
+            if vc > 0:
+                group_p_part(e, h, 0, vc, nc.vector.tensor_copy)
+            if vc < F:
+                group_p_part(e, h, vc, F, nc.scalar.copy)
+
+        def group_p_part(e, h, f0, f1, copy):
             if (e, h) not in p_grp:
                 p_grp[e, h] = work.tile([P, F, 4], BF16, name="p_grp", tag="grp", bufs=5, align_bytes=64)
-            f0 = 256 * part
-            dst = p_grp[e, h][:, f0 : f0 + 256, :]
-            src = p_raw[e, h][:, :, f0 : f0 + 256].rearrange("p t f -> p f t")
-            if part == 0:
-                nc.vector.tensor_copy(out=dst, in_=src)
-            else:
-                nc.scalar.copy(out=dst, in_=src)
+            dst = p_grp[e, h][:].rearrange("p (f i) t -> p f t i", i=4)
+            src = p_raw[e, h][:].rearrange("p t (f i) -> p f t i", i=4)
+            copy(out=dst[:, f0 // 4 : f1 // 4], in_=src[:, f0 // 4 : f1 // 4])
 
         def quant_p(e, h):
             p_codes[e, h] = work.tile([P, F], U32, name="p_codes", tag="p_codes", bufs=5, align_bytes=64)
@@ -182,23 +199,22 @@ def tile_relationalgraphmixtureofexperts_x2_kernel(tc, x, a, w, c, b, wg, w0_wor
 
         agg, proj0 = {}, {}
 
-        def aggregate(s):
-            v, e, g = s // 2, s // 4, (s // 2) % 2
-            for q in (2 * (s % 2), 2 * (s % 2) + 1):
-                agg[v, q] = psum.tile([P, 512], F32, name="ag", tag="ag", bufs=3)
-                for h in range(2):
-                    if FORM[e] == "a":
-                        fs = slice(128 * q, 128 * q + 128)
-                        lhs = (p_codes[e, h][:, fs], p_sc[e, h][:, fs])
-                        rhs = (a_codes[v][:, 512 * h : 512 * h + 512], a_sc[v][:, 512 * h : 512 * h + 512])
-                    else:
-                        ns = slice(512 * h + 128 * q, 512 * h + 128 * q + 128)
-                        lhs = (a_codes[v][:, ns], a_sc[v][:, ns])
-                        rhs = (p_codes[e, h][:], p_sc[e, h][:])
-                    mx(agg[v, q][:], lhs, rhs, h == 0, h == 1)
-                if e == PLAIN[0]:
-                    proj0[v, q] = psum.tile([P, 512], F32, name="ag", tag="ag", bufs=3)
-                    mx(proj0[v, q][:], x_tile(4 * g + q), (w0_codes[:], w0_sc[:]), True, True)
+        def aggregate(v, q):
+            e, g = v // 2, v % 2
+            agg[v, q] = psum.tile([P, 512], F32, name="ag", tag="ag", bufs=4)
+            for h in range(2):
+                if FORM[e] == "a":
+                    fs = slice(128 * q, 128 * q + 128)
+                    lhs = (p_codes[e, h][:, fs], p_sc[e, h][:, fs])
+                    rhs = (a_codes[v][:, 512 * h : 512 * h + 512], a_sc[v][:, 512 * h : 512 * h + 512])
+                else:
+                    ns = slice(512 * h + 128 * q, 512 * h + 128 * q + 128)
+                    lhs = (a_codes[v][:, ns], a_sc[v][:, ns])
+                    rhs = (p_codes[e, h][:], p_sc[e, h][:])
+                mx(agg[v, q][:], lhs, rhs, h == 0, h == 1)
+            if e == PLAIN[0]:
+                proj0[v, q] = psum.tile([P, 512], F32, name="ag", tag="ag", bufs=4)
+                mx(proj0[v, q][:], x_tile(4 * g + q), (w0_codes[:], w0_sc[:]), True, True)
 
         acc = keep.tile([P, 8, F], F32, name="acc", align_bytes=64)
         u_t, turned, res, sums = {}, {}, {}, {}
@@ -208,15 +224,17 @@ def tile_relationalgraphmixtureofexperts_x2_kernel(tc, x, a, w, c, b, wg, w0_wor
             nc.vector.tensor_tensor(out=u_t[v, q][:], in0=agg[v, q][:], in1=nb[v // 2][:], op=ALU.max)
 
         def result(i):
-            if i % 4 == 0:
+            if i % 4 == 0 and i // 4 not in res:
                 res[i // 4] = work.tile([P, 4, F], F32, name="res", tag="big", bufs=5, align_bytes=64)
             return res[i // 4][:, i % 4, :]
 
-        def weigh(v, q):
+        def weigh(v, q, f0=0, f1=F):
             e, i = v // 2, 4 * (v % 2) + q
             other = proj0[v, q][:] if e == PLAIN[0] else acc[:, i, :]
             dst = result(i) if e == E - 1 else acc[:, i, :]
-            nc.vector.scalar_tensor_tensor(out=dst, in0=u_t[v, q][:], scalar=gate[:, i, e : e + 1], in1=other, op0=ALU.mult, op1=ALU.add)
+            nc.vector.scalar_tensor_tensor(
+                out=dst[:, f0:f1], in0=u_t[v, q][:, f0:f1], scalar=gate[:, i, e : e + 1], in1=other[:, f0:f1], op0=ALU.mult, op1=ALU.add
+            )
 
         def clamp_weigh(v, q):
             e, g = v // 2, v % 2
@@ -226,10 +244,10 @@ def tile_relationalgraphmixtureofexperts_x2_kernel(tc, x, a, w, c, b, wg, w0_wor
                 out=turned[v][:, q, :], in0=agg[v, q][:], scalar=nb_col[:, q, e : e + 1], in1=g_rows[e][:, 512 * g : 512 * g + 512], op0=ALU.max, op1=ALU.mult
             )
 
-        def turn_back(i):
+        def turn_back(i, tag="ag", bufs=4):
             g, t = i // 4, i % 4
-            sums[i] = psum.tile([P, 512], F32, name="ag", tag="ag", bufs=3)
-            nc.tensor.matmul(out=sums[i][:], lhsT=g_t[:, i, :], rhs=b_rows[:], start=True, stop=False)
+            sums[i] = psum.tile([P, 512], F32, name=tag, tag=tag, bufs=bufs)
+            nc.tensor.matmul(out=sums[i][:], lhsT=g_t[:, i, :], rhs=b_rows[:], start=True, stop=not TURNED)
             for e in TURNED:
                 for q in range(4):
                     nc.tensor.matmul(
@@ -242,110 +260,67 @@ def tile_relationalgraphmixtureofexperts_x2_kernel(tc, x, a, w, c, b, wg, w0_wor
                     )
 
         def add_turned(i):
-            dst = acc[:, i, :] if TURNED[-1] < E - 1 else result(i)
+            dst = acc[:, i, :] if max(TURNED + [0]) < E - 1 else result(i)
             nc.vector.tensor_tensor(out=dst, in0=sums[i][:], in1=acc[:, i, :], op=ALU.add)
 
-        def store(g, half):
-            nc.sync.dma_start(
-                out=out_0[512 * g : 512 * g + 512, :].rearrange("(p t) m -> p t m", t=4)[:, 2 * half : 2 * half + 2, :],
-                in_=res[g][:, 2 * half : 2 * half + 2, :],
-            )
+        def store(i):
+            g, t = i // 4, i % 4
+            nc.sync.dma_start(out=out_0[512 * g : 512 * g + 512, :].rearrange("(p t) m -> p t m", t=4)[:, t, :], in_=res[g][:, t, :])
 
-        def finish(g):
-            grp = work.tile([P, F, 4], BF16, name="o_grp", tag="grp", bufs=5, align_bytes=64)
-            codes = work.tile([P, F], U32, name="o_codes", tag="p_codes", bufs=5, align_bytes=64)
-            scs = work.tile([P, F], U8, name="o_sc", tag="p_sc", bufs=5, align_bytes=64)
-            for part in range(2):
-                f0 = 256 * part
-                dst = grp[:, f0 : f0 + 256, :]
-                src = res[g][:, :, f0 : f0 + 256].rearrange("p t f -> p f t")
-                if part == 0:
-                    nc.vector.tensor_copy(out=dst, in_=src)
-                else:
-                    nc.scalar.copy(out=dst, in_=src)
-            for part in range(2):
-                f0 = 256 * part
-                nc.vector.quantize_mx(
-                    out=codes[:, f0 : f0 + 256].bitcast(FP8X4), scales=scs[:, f0 : f0 + 256], in_=grp[:, f0 : f0 + 256, :].rearrange("p f t -> p (f t)")
-                )
-            nc.sync.dma_start(out=out_1[g].rearrange("p m t -> p (m t)").bitcast(I32), in_=codes[:].bitcast(I32))
+        o_grp, o_codes, o_sc = {}, {}, {}
+
+        def round_out(g, part, on_vector):
+            if g not in o_grp:
+                o_grp[g] = work.tile([P, F, 4], BF16, name="o_grp", tag="grp", bufs=5, align_bytes=64)
+                o_codes[g] = work.tile([P, F], U32, name="o_codes", tag="p_codes", bufs=5, align_bytes=64)
+                o_sc[g] = work.tile([P, F], U8, name="o_sc", tag="p_sc", bufs=5, align_bytes=64)
+            f0 = 256 * part
+            dst = o_grp[g][:, f0 : f0 + 256, :].rearrange("p (f i) t -> p f t i", i=4)
+            src = res[g][:, :, f0 : f0 + 256].rearrange("p t (f i) -> p f t i", i=4)
+            if on_vector:
+                nc.vector.tensor_copy(out=dst, in_=src)
+            else:
+                nc.scalar.copy(out=dst, in_=src)
+
+        def quant_out(g, part):
+            cols = slice(256 * part, 256 * part + 256)
+            nc.vector.quantize_mx(out=o_codes[g][:, cols].bitcast(FP8X4), scales=o_sc[g][:, cols], in_=o_grp[g][:, cols, :].rearrange("p f t -> p (f t)"))
+
+        def store_planes(g):
+            nc.sync.dma_start(out=out_1[g].rearrange("p m t -> p (m t)").bitcast(I32), in_=o_codes[g][:].bitcast(I32))
             for q in range(4):
-                nc.sync.dma_start(out=out_2[g, 4 * q : 4 * q + 4, :].bitcast(I32), in_=scs[32 * q : 32 * q + 4, :].bitcast(I32))
+                nc.sync.dma_start(out=out_2[g, 4 * q : 4 * q + 4, :].bitcast(I32), in_=o_sc[g][32 * q : 32 * q + 4, :].bitcast(I32))
 
-        turn_x(0)
-        group_w(0)
-        quant_w(0)
-        quant_x(0)
-        turn_x(1)
-        zps = psum.tile([P, 512], F32, name="ag", tag="ag", bufs=3)
+        def small(name, shape):
+            return keep.tile(shape, F32, name=name, align_bytes=64)
 
-        def gate_logits(g):
+        c_f = small("c_f", [P, 8])
+        nb_col = small("nb_col", [P, 4, E])
+        zmax, zsum, zrec = small("zmax", [P, 8]), small("zsum", [P, 8]), small("zrec", [P, 8])
+        zs, ez, gate = small("zs", [P, 8, E]), small("ez", [P, 8, E]), small("gate", [P, 8, E])
+        r1, r2 = small("r1", [P, 8, E]), small("r2", [P, 8, E])
+        g_rows = {e: small("g_rows%d" % e, [P, N]) for e in TURNED}
+        g_t = keep.tile([P, 8, P], BF16, name="g_t", align_bytes=64)
+
+        def gate_logits(zps, g):
             for i in range(4 * g, 4 * g + 4):
                 xs = x_t[:, 512 * i : 512 * i + 512].rearrange("p (n j) -> p n j", j=4)
                 for j in range(4):
                     nc.tensor.matmul(out=zps[:, 4 * i : 4 * i + 4], lhsT=xs[:, :, j], rhs=wg_sb[:, j, :], start=(j == 0), stop=(j == 3))
 
-        nb_col = keep.tile([P, 4, E], F32, name="nb_col", align_bytes=64)
-        nb_bank = psum.tile([P, 4, P], BF16, name="tp", tag="tp", bufs=3)
-        for q in range(4):
-            nc.tensor.transpose(nb_bank[:, q, :], b_rows[:, 128 * q : 128 * q + 128], ident_bf[:])
-        nc.scalar.activation(out=nb_col[:], in_=nb_bank[:, :, 0:E], func=ACT.Copy, scale=-1.0)
-
-        gate_logits(0)
-        quant_x(1)
-        gate_logits(1)
-        for i in range(4):
-            project(0, i, i % 2 == 1)
-        z = zps[:, 0:32].rearrange("p (i e) -> p i e", e=E)
-        zmax = keep.tile([P, 8], F32, name="zmax", align_bytes=64)
-        nc.vector.reduce_max(out=zmax[:], in_=z, axis=AX.X)
-        zs = keep.tile([P, 8, E], F32, name="zs", align_bytes=64)
-        nc.vector.tensor_tensor(out=zs[:], in0=z, in1=zmax[:].unsqueeze(2).to_broadcast([P, 8, E]), op=ALU.subtract)
-        ez = keep.tile([P, 8, E], F32, name="ez", align_bytes=64)
-        nc.scalar.activation(out=ez[:], in_=zs[:], func=ACT.Exp)
-        turn_a(0)
-        group_p(0, 0, 0)
-        group_p(0, 0, 1)
-        zsum = keep.tile([P, 8], F32, name="zsum", align_bytes=64)
-        nc.vector.reduce_sum(out=zsum[:], in_=ez[:], axis=AX.X)
-        for i in range(4, 8):
-            project(0, i, i % 2 == 1)
-        zrec = keep.tile([P, 8], F32, name="zrec", align_bytes=64)
-        nc.vector.reciprocal(out=zrec[:], in_=zsum[:])
-        turn_a(1)
-        gate = keep.tile([P, 8, E], F32, name="gate", align_bytes=64)
-        nc.vector.tensor_tensor(out=gate[:], in0=ez[:], in1=zrec[:].unsqueeze(2).to_broadcast([P, 8, E]), op=ALU.mult)
-        quant_p(0, 0)
-        g_rows = {}
-        for e in TURNED:
-            g_rows[e] = keep.tile([P, N], F32, name="g_rows%d" % e, align_bytes=64)
+        def bias_columns():
+            bank = psum.tile([P, 4, P], BF16, name="tp", tag="tp", bufs=2)
+            for q in range(4):
+                nc.tensor.transpose(bank[:, q, :], b_rows[:, 128 * q : 128 * q + 128], ident_bf[:])
+            nc.scalar.activation(out=nb_col[:], in_=bank[:, :, 0:E], func=ACT.Copy, scale=-1.0)
 
         def spread_gate(e, g):
-            bank = psum.tile([P, 512], F32, name="tp", tag="tp", bufs=3)
+            bank = psum.tile([P, 512], F32, name="tp", tag="tp", bufs=2)
             for t in range(4):
                 nc.tensor.transpose(bank[:, 128 * t : 128 * t + 128], gate[:, 4 * g + t, e : e + 1].to_broadcast([P, P]), ident[:])
             nc.scalar.copy(out=g_rows[e][:, 512 * g : 512 * g + 512], in_=bank[:])
 
-        spread_gate(0, 0)
-        group_p(0, 1, 0)
-        group_p(0, 1, 1)
-        quant_a(0, 0)
-        quant_a(0, 1)
-        quant_p(0, 1)
-        for e in PLAIN:
-            nb[e] = keep.tile([P, F], BF16, name="nb%d" % e, align_bytes=64)
-            nc.vector.tensor_scalar(out=nb[e][:], in0=b_bc[e][:], scalar1=-1.0, scalar2=None, op0=ALU.mult)
-        group_w(1)
-        quant_w(1)
-        project(1, 0, False)
-        project(1, 1, False)
-        turn_a(2)
-
-        g_t = keep.tile([P, 8, P], BF16, name="g_t", align_bytes=64)
-
         def split_gate():
-            r1 = keep.tile([P, 8, E], F32, name="g_r1", align_bytes=64)
-            r2 = keep.tile([P, 8, E], F32, name="g_r2", align_bytes=64)
             nc.vector.tensor_copy(out=g_parts[:, :, 0:4], in_=gate[:])
             nc.vector.tensor_tensor(out=r1[:], in0=gate[:], in1=g_parts[:, :, 0:4], op=ALU.subtract)
             nc.vector.tensor_copy(out=g_parts[:, :, 4:8], in_=r1[:])
@@ -353,66 +328,174 @@ def tile_relationalgraphmixtureofexperts_x2_kernel(tc, x, a, w, c, b, wg, w0_wor
             nc.vector.tensor_copy(out=g_parts[:, :, 8:12], in_=r2[:])
 
         def turn_gate():
-            bank = psum.tile([P, 8, P], BF16, name="tp", tag="tp", bufs=3)
+            bank = psum.tile([P, 8, P], BF16, name="tp", tag="tp", bufs=2)
             for i in range(8):
                 nc.tensor.transpose(bank[:, i, :], g_parts[:, i, :], ident_bf[:])
             nc.scalar.copy(out=g_t[:], in_=bank[:])
 
-        spread_at = {1: [(0, 1)], 2: [(e, 0) for e in TURNED[1:]], 3: [(e, 1) for e in TURNED[1:]]}
-        back_at = {}
-        for g in range(2):
-            for half in range(2):
-                back_at[4 * TURNED[-1] + 2 * g + 2 + half] = [4 * g + 2 * half, 4 * g + 2 * half + 1]
-        for s in range(STEPS + 2):
+        def negate_bias(e):
+            nb[e] = keep.tile([P, F], BF16, name="nb%d" % e, align_bytes=64)
+            nc.vector.tensor_scalar(out=nb[e][:], in0=b_bc[e][:], scalar1=-1.0, scalar2=None, op0=ALU.mult)
+
+        LEAD, PLEAD = 3, 2
+        ctx.enter_context(tc.manual_schedule(engines={mybir.EngineType.PE}))
+        spread_at = {}
+        back_at = {5: [0, 1], 6: [2, 3], 7: [4, 5], 8: [6, 7]}
+        hot = psum.tile([P, 512], F32, name="ag", tag="ag", bufs=4)
+
+        def warm(n):
+            for i in range(n):
+                nc.tensor.matmul(out=hot[:], lhsT=zeros[:, 0:P], rhs=zeros[:], start=True, stop=True)
+
+        nc.scalar.activation(out=zs[:, 0, :], in_=zeros[:, 0:E], func=ACT.Exp)
+        warm(6)
+        turn_x(0)
+        warm(3)
+        turn_x(1, True)
+        warm(2)
+        group_w(0)
+        nc.vector.tensor_copy(out=c_f[:], in_=c_bf[:].rearrange("p h t -> p (h t)"))
+        quant_w(0)
+        quant_x(0)
+        turn_x_copy(1, 1, nc.vector.tensor_copy)
+        HP = {0: ("pp", 2), 1: ("pp", 2), 2: ("ag", 4), 3: ("ag", 4), 4: ("ag", 4), 5: ("pp", 2), 6: ("pp", 2), 7: ("ag", 4)}
+        for i in range(4):
+            project(0, i, *HP[i])
+        scale_p(0, 0)
+        scale_p(0, 2)
+        quant_x(1)
+        scale_p(0, 1, True)
+        scale_p(0, 3, True)
+        turn_a(0, 0)
+        group_p_part(0, 0, 256, F, nc.scalar.copy)
+        group_p_part(0, 0, 0, 256, nc.vector.tensor_copy)
+        turn_a(0, 1)
+        for i in range(4, 8):
+            project(0, i, *HP[i])
+        scale_p(0, 4)
+        scale_p(0, 5, True)
+        scale_p(0, 6)
+        scale_p(0, 7, True)
+        quant_p(0, 0)
+        turn_a(1, 0)
+        group_p_part(0, 1, 256, F, nc.scalar.copy)
+        group_p_part(0, 1, 0, 256, nc.vector.tensor_copy)
+        turn_a(1, 1)
+        quant_p(0, 1)
+        quant_a(0, 0)
+        quant_a(0, 1)
+        zps = psum.tile([P, 512], F32, name="ag", tag="ag", bufs=4)
+        gate_logits(zps, 0)
+        gate_logits(zps, 1)
+        z = zps[:, 0:32].rearrange("p (i e) -> p i e", e=E)
+        turn_a(2, 0)
+        turn_a(2, 1)
+        negate_bias(0)
+        nc.vector.reduce_max(out=zmax[:], in_=z, axis=AX.X)
+        group_w(1)
+        nc.vector.tensor_tensor(out=zs[:], in0=z, in1=zmax[:].unsqueeze(2).to_broadcast([P, 8, E]), op=ALU.subtract)
+        nc.scalar.activation(out=ez[:], in_=zs[:], func=ACT.Exp)
+        quant_w(1)
+        nc.vector.reduce_sum(out=zsum[:], in_=ez[:], axis=AX.X)
+
+        def epilogue_1(u, q):
+            (clamp if FORM[u // 2] == "n" else clamp_weigh)(u, q)
+
+        for s in range(STEPS + 1):
             v, e, j = s // 2, s // 4, s % 4
-            if s < STEPS:
-                aggregate(s)
-                k, pe = (s + 1) % 4, (s + 1) // 4 + 1
-                if pe < E:
-                    project(pe, 2 * k, False)
-                    project(pe, 2 * k + 1, False)
-            for i in back_at.get(s, []):
-                turn_back(i)
+            q0, q1 = 2 * (s % 2), 2 * (s % 2) + 1
+            pv, pe = (s - 1) // 2, (s - 1) // 4
+            pq0, pq1 = 2 * ((s - 1) % 2), 2 * ((s - 1) % 2) + 1
+            plain = s >= 1 and FORM[pe] == "n"
+            turn = s + LEAD
+            turns = 0 <= turn < STEPS
+            ne = max(e + 1 if j < 3 else e + 2, 1)
+            pairs = {-1: [], 0: [0, 1], 1: [2], 2: [3]}[s] if s < 3 else [(j + 1) % 4]
+            gp, gh = e + 1, j // 2
+            group = j % 2 == 1 and gp < E and s < STEPS
+            quant = j >= 2 and gp < E and s < STEPS
+            share = VC if gp > 0 else 320
+            if group and share < F:
+                group_p_part(gp, gh, share, F, nc.scalar.copy)
+            for piece in "ATP":
+                if piece == "A" and 0 <= s < STEPS:
+                    aggregate(v, q0)
+                    aggregate(v, q1)
+                if piece == "a" and 0 <= s < STEPS:
+                    aggregate(v, q0)
+                if piece == "b" and 0 <= s < STEPS:
+                    aggregate(v, q1)
+                if piece == "T" and turns:
+                    turn_a(turn, 0)
+                    turn_a(turn, 1)
+                if piece == "t" and turns:
+                    turn_a(turn, 0)
+                if piece == "u" and turns:
+                    turn_a(turn, 1)
+                if piece == "P" and ne < E and s < STEPS:
+                    for k in pairs:
+                        for i in (2 * k, 2 * k + 1):
+                            project(ne, i)
+                            scale_p(ne, i)
+                if piece == "B":
+                    for i in back_at.get(s, []):
+                        turn_back(i)
+            if "B" not in "ATP":
+                for i in back_at.get(s, []):
+                    turn_back(i)
             for ee, g in spread_at.get(s, []):
                 spread_gate(ee, g)
-            if s + 3 < STEPS:
-                turn_a(s + 3)
+            if s == 3 and TURNED:
+                bias_columns()
             if s == 4:
-                split_gate()
                 turn_gate()
-            if s >= STEPS:
-                for i in back_at.get(s, []):
-                    add_turned(i)
-                continue
-            if j == 3 and e + 1 < E:
-                group_p(e + 1, 1, 0)
-                group_p(e + 1, 1, 1)
-            q0, q1 = 2 * (s % 2), 2 * (s % 2) + 1
-            first = clamp if FORM[e] == "n" else clamp_weigh
-            first(v, q0)
-            if s % 2 == 1 and v + 1 < 8:
-                quant_a(v + 1, 0)
-            first(v, q1)
-            if s % 2 == 1 and v + 1 < 8:
-                quant_a(v + 1, 1)
-            if j == 3 and e + 1 < E:
-                quant_p(e + 1, 1)
-            if j == 2 and e + 1 < E:
-                quant_p(e + 1, 0)
-            if FORM[e] == "n":
-                weigh(v, q0)
-            if j == 0 and e + 2 < E:
-                group_w(e + 2)
-            if j == 1 and e + 1 < E:
-                group_p(e + 1, 0, 0)
-                group_p(e + 1, 0, 1)
-            if j == 1 and e + 2 < E:
-                quant_w(e + 2)
-            if FORM[e] == "n":
-                weigh(v, q1)
+            if s >= 1:
+                epilogue_1(pv, pq0)
+            if group and share > 0:
+                group_p_part(gp, gh, 0, share, nc.vector.tensor_copy)
+            if s >= 1:
+                epilogue_1(pv, pq1)
+            if s == 0:
+                nc.vector.reciprocal(out=zrec[:], in_=zsum[:])
+            if s % 2 == 1 and 0 <= (s - 1) // 2 + 1 < 8:
+                quant_a((s - 1) // 2 + 1, 0)
+            if plain:
+                weigh(pv, pq0)
+            if s == 0:
+                nc.vector.tensor_tensor(out=gate[:], in0=ez[:], in1=zrec[:].unsqueeze(2).to_broadcast([P, 8, E]), op=ALU.mult)
+            if s % 2 == 1 and 0 <= (s - 1) // 2 + 1 < 8:
+                quant_a((s - 1) // 2 + 1, 1)
+            if quant:
+                quant_p(gp, j - 2)
+            if s == 1 or s == 5:
+                group_w(2 if s == 1 else 3)
+            if plain:
+                if s == STEPS:
+                    weigh(pv, pq1, 0, 256)
+                    round_out(1, 0, False)
+                    weigh(pv, pq1, 256, 512)
+                else:
+                    weigh(pv, pq1)
+            if s == 2 or s == 6:
+                quant_w(2 if s == 2 else 3)
+            if s == 2:
+                split_gate()
+            if s == 3:
+                for ee in PLAIN[1:]:
+                    negate_bias(ee)
             for i in back_at.get(s, []):
                 add_turned(i)
-            if e == 3 and FORM[3] == "n":
-                store(j // 2, j % 2)
-                if j % 2 == 1:
-                    finish(j // 2)
+            if pe == E - 1 and s >= 1:
+                store(4 * (pv % 2) + pq0)
+                store(4 * (pv % 2) + pq1)
+            if s == STEPS - 1:
+                round_out(0, 0, True)
+                round_out(0, 1, False)
+                quant_out(0, 0)
+                quant_out(0, 1)
+                store_planes(0)
+            if s == STEPS:
+                round_out(1, 1, True)
+                quant_out(1, 1)
+                quant_out(1, 0)
+                store_planes(1)

@@ -17,10 +17,11 @@ N, D, F, E = 1024, 512, 512, 4
 P = 128
 FLOPS = 2 * (E * N * D * F + E * N * N * F + N * D * F)
 STEPS = 16
-FORM = "nnnn"
+FORM = "nnnr"
 TURNED = [e for e in range(E) if FORM[e] == "a"]
 PLAIN = [e for e in range(E) if FORM[e] == "n"]
-VC = 0
+LAST = E - 1
+VC = 64
 
 
 def tile_relationalgraphmixtureofexperts_x2_kernel(tc, x, a, w, c, b, wg, w0_words, w0_scales, out_0, out_1, out_2):
@@ -48,7 +49,7 @@ def tile_relationalgraphmixtureofexperts_x2_kernel(tc, x, a, w, c, b, wg, w0_wor
         c_bf = keep.tile([P, 2, 4], BF16, name="c_bf", align_bytes=64)
         wg_sb = keep.tile([P, 4, E], BF16, name="wg_sb", align_bytes=64)
         x_raw, w_raw, a_raw = {}, {}, {}
-        b_bc, nb = {}, {}
+        nb = {}
 
         def load_x(g):
             x_raw[g] = work.tile([P, 4, D], BF16, name="x_raw", tag="raw", bufs=12, align_bytes=64)
@@ -64,29 +65,24 @@ def tile_relationalgraphmixtureofexperts_x2_kernel(tc, x, a, w, c, b, wg, w0_wor
             a_raw[s] = work.tile([P, 2, N], BF16, name="a_raw", tag="raw", bufs=12, align_bytes=64)
             nc.sync.dma_start(out=a_raw[s][:], in_=src[:, 2 * h : 2 * h + 2, :])
 
+        nc.scalar.dma_start(out=c_bf[:], in_=c.rearrange("(h p t) -> p h t", p=P, t=4))
+        nc.scalar.dma_start(out=wg_sb[:], in_=wg.rearrange("(p t) e -> p t e", t=4))
+        for j in range(3):
+            nc.scalar.dma_start(out=b_rows[4 * j : 4 * j + 4, :], in_=b)
         load_x(0)
         load_w(0)
-        nc.sync.dma_start(out=c_bf[:], in_=c.rearrange("(h p t) -> p h t", p=P, t=4))
-        nc.sync.dma_start(out=wg_sb[:], in_=wg.rearrange("(p t) e -> p t e", t=4))
         load_x(1)
-        load_a(0)
         load_w(1)
+        load_a(0)
         load_a(1)
-        for e in PLAIN:
-            b_bc[e] = keep.tile([P, F], BF16, name="b_bc%d" % e, align_bytes=64)
-        nc.sync.dma_start(out=b_bc[0][:], in_=b[0].partition_broadcast(P))
         nc.sync.dma_start(out=w0_codes[:].bitcast(I32), in_=w0_words[0].rearrange("p n t -> p (n t)").bitcast(I32))
         for q in range(4):
             nc.sync.dma_start(out=w0_sc[32 * q : 32 * q + 4, :].bitcast(I32), in_=w0_scales[0, 4 * q : 4 * q + 4, :].bitcast(I32))
         load_a(2)
         load_a(3)
-        for j in range(3):
-            nc.sync.dma_start(out=b_rows[4 * j : 4 * j + 4, :], in_=b)
         load_w(2)
         for s in range(4, 8):
             load_a(s)
-        for e in PLAIN[1:]:
-            nc.sync.dma_start(out=b_bc[e][:], in_=b[e].partition_broadcast(P))
         load_w(3)
         for s in range(8, STEPS):
             load_a(s)
@@ -100,7 +96,7 @@ def tile_relationalgraphmixtureofexperts_x2_kernel(tc, x, a, w, c, b, wg, w0_wor
         def turn_x(g, hold=False):
             words = x_raw[g][:].rearrange("p t k -> p (t k)").bitcast(F32)
             for half in range(2):
-                bank = psum.tile([P, 512], F32, name="tp", tag="tp", bufs=2)
+                bank = psum.tile([P, 512], F32, name="tp", tag="tp", bufs=3)
                 x_bank[g, half] = bank
                 for tt in range(2):
                     for u in range(2):
@@ -139,7 +135,7 @@ def tile_relationalgraphmixtureofexperts_x2_kernel(tc, x, a, w, c, b, wg, w0_wor
             if half == 0 and tt == 0:
                 a_t[v] = work.tile([P, 4096], BF16, name="a_t", tag="a_t", bufs=3, align_bytes=64)
             dst = a_t[v][:].bitcast(F32).rearrange("p (h t n u) -> p h t n u", h=2, t=4, u=2)
-            bank = psum.tile([P, 512], F32, name="tp", tag="tp", bufs=2)
+            bank = psum.tile([P, 512], F32, name="tp", tag="tp", bufs=3)
             for h in range(2):
                 for u in range(2):
                     lo = 512 * tt + 256 * h + u
@@ -201,9 +197,9 @@ def tile_relationalgraphmixtureofexperts_x2_kernel(tc, x, a, w, c, b, wg, w0_wor
 
         def aggregate(v, q):
             e, g = v // 2, v % 2
-            agg[v, q] = psum.tile([P, 512], F32, name="ag", tag="ag", bufs=4)
+            agg[v, q] = psum.tile([P, 512], F32, name="ag", tag="ag", bufs=3)
             for h in range(2):
-                if FORM[e] == "a":
+                if FORM[e] != "n":
                     fs = slice(128 * q, 128 * q + 128)
                     lhs = (p_codes[e, h][:, fs], p_sc[e, h][:, fs])
                     rhs = (a_codes[v][:, 512 * h : 512 * h + 512], a_sc[v][:, 512 * h : 512 * h + 512])
@@ -213,7 +209,7 @@ def tile_relationalgraphmixtureofexperts_x2_kernel(tc, x, a, w, c, b, wg, w0_wor
                     rhs = (p_codes[e, h][:], p_sc[e, h][:])
                 mx(agg[v, q][:], lhs, rhs, h == 0, h == 1)
             if e == PLAIN[0]:
-                proj0[v, q] = psum.tile([P, 512], F32, name="ag", tag="ag", bufs=4)
+                proj0[v, q] = psum.tile([P, 512], F32, name="ag", tag="ag", bufs=3)
                 mx(proj0[v, q][:], x_tile(4 * g + q), (w0_codes[:], w0_sc[:]), True, True)
 
         acc = keep.tile([P, 8, F], F32, name="acc", align_bytes=64)
@@ -223,9 +219,27 @@ def tile_relationalgraphmixtureofexperts_x2_kernel(tc, x, a, w, c, b, wg, w0_wor
             u_t[v, q] = work.tile([P, F], F32, name="u_t", tag="u_t", bufs=4, align_bytes=64)
             nc.vector.tensor_tensor(out=u_t[v, q][:], in0=agg[v, q][:], in1=nb[v // 2][:], op=ALU.max)
 
+        def relu_turned(v, q):
+            if q == 0:
+                turned[v] = work.tile([P, 4, F], F32, name="turned", tag="big", bufs=4, align_bytes=64)
+            nc.scalar.activation(out=turned[v][:, q, :], in_=agg[v, q][:], func=ACT.Relu, bias=nb_col[:, q, LAST : LAST + 1])
+
+        def turn_node_tile(v, t, qs, tag, bufs):
+            i = 4 * (v % 2) + t
+            if 0 in qs:
+                sums[i] = psum.tile([P, 512], F32, name=tag, tag=tag, bufs=bufs)
+            for q in qs:
+                nc.tensor.transpose(sums[i][:, 128 * q : 128 * q + 128], turned[v][:, q, 128 * t : 128 * t + 128], ident[:])
+
+        def weigh_turned(v, t):
+            i = 4 * (v % 2) + t
+            nc.vector.scalar_tensor_tensor(
+                out=result(i), in0=sums[i][:], scalar=gate[:, i, LAST : LAST + 1], in1=acc[:, i, :], op0=ALU.mult, op1=ALU.add
+            )
+
         def result(i):
             if i % 4 == 0 and i // 4 not in res:
-                res[i // 4] = work.tile([P, 4, F], F32, name="res", tag="big", bufs=5, align_bytes=64)
+                res[i // 4] = work.tile([P, 4, F], F32, name="res", tag="big", bufs=4, align_bytes=64)
             return res[i // 4][:, i % 4, :]
 
         def weigh(v, q, f0=0, f1=F):
@@ -239,12 +253,12 @@ def tile_relationalgraphmixtureofexperts_x2_kernel(tc, x, a, w, c, b, wg, w0_wor
         def clamp_weigh(v, q):
             e, g = v // 2, v % 2
             if q == 0:
-                turned[v] = work.tile([P, 4, F], F32, name="turned", tag="big", bufs=5, align_bytes=64)
+                turned[v] = work.tile([P, 4, F], F32, name="turned", tag="big", bufs=4, align_bytes=64)
             nc.vector.scalar_tensor_tensor(
                 out=turned[v][:, q, :], in0=agg[v, q][:], scalar=nb_col[:, q, e : e + 1], in1=g_rows[e][:, 512 * g : 512 * g + 512], op0=ALU.max, op1=ALU.mult
             )
 
-        def turn_back(i, tag="ag", bufs=4):
+        def turn_back(i, tag="ag", bufs=3):
             g, t = i // 4, i % 4
             sums[i] = psum.tile([P, 512], F32, name=tag, tag=tag, bufs=bufs)
             nc.tensor.matmul(out=sums[i][:], lhsT=g_t[:, i, :], rhs=b_rows[:], start=True, stop=not TURNED)
@@ -260,7 +274,7 @@ def tile_relationalgraphmixtureofexperts_x2_kernel(tc, x, a, w, c, b, wg, w0_wor
                     )
 
         def add_turned(i):
-            dst = acc[:, i, :] if max(TURNED + [0]) < E - 1 else result(i)
+            dst = acc[:, i, :]
             nc.vector.tensor_tensor(out=dst, in0=sums[i][:], in1=acc[:, i, :], op=ALU.add)
 
         def store(i):
@@ -309,39 +323,43 @@ def tile_relationalgraphmixtureofexperts_x2_kernel(tc, x, a, w, c, b, wg, w0_wor
                     nc.tensor.matmul(out=zps[:, 4 * i : 4 * i + 4], lhsT=xs[:, :, j], rhs=wg_sb[:, j, :], start=(j == 0), stop=(j == 3))
 
         def bias_columns():
-            bank = psum.tile([P, 4, P], BF16, name="tp", tag="tp", bufs=2)
+            bank = psum.tile([P, 4, P], BF16, name="tp", tag="tp", bufs=3)
             for q in range(4):
                 nc.tensor.transpose(bank[:, q, :], b_rows[:, 128 * q : 128 * q + 128], ident_bf[:])
-            nc.scalar.activation(out=nb_col[:], in_=bank[:, :, 0:E], func=ACT.Copy, scale=-1.0)
+            nc.scalar.activation(out=nb_col[:, :, 0:LAST], in_=bank[:, :, 0:LAST], func=ACT.Copy, scale=-1.0)
+            nc.scalar.activation(out=nb_col[:, :, LAST:E], in_=bank[:, :, LAST:E], func=ACT.Copy)
 
         def spread_gate(e, g):
-            bank = psum.tile([P, 512], F32, name="tp", tag="tp", bufs=2)
+            bank = psum.tile([P, 512], F32, name="tp", tag="tp", bufs=3)
             for t in range(4):
                 nc.tensor.transpose(bank[:, 128 * t : 128 * t + 128], gate[:, 4 * g + t, e : e + 1].to_broadcast([P, P]), ident[:])
             nc.scalar.copy(out=g_rows[e][:, 512 * g : 512 * g + 512], in_=bank[:])
 
         def split_gate():
-            nc.vector.tensor_copy(out=g_parts[:, :, 0:4], in_=gate[:])
-            nc.vector.tensor_tensor(out=r1[:], in0=gate[:], in1=g_parts[:, :, 0:4], op=ALU.subtract)
-            nc.vector.tensor_copy(out=g_parts[:, :, 4:8], in_=r1[:])
-            nc.vector.tensor_tensor(out=r2[:], in0=r1[:], in1=g_parts[:, :, 4:8], op=ALU.subtract)
-            nc.vector.tensor_copy(out=g_parts[:, :, 8:12], in_=r2[:])
+            n = len(PLAIN) + len(TURNED)
+            nc.vector.tensor_copy(out=g_parts[:, :, 0:n], in_=gate[:, :, 0:n])
+            nc.vector.tensor_tensor(out=r1[:, :, 0:n], in0=gate[:, :, 0:n], in1=g_parts[:, :, 0:n], op=ALU.subtract)
+            nc.vector.tensor_copy(out=g_parts[:, :, 4 : 4 + n], in_=r1[:, :, 0:n])
+            nc.vector.tensor_tensor(out=r2[:, :, 0:n], in0=r1[:, :, 0:n], in1=g_parts[:, :, 4 : 4 + n], op=ALU.subtract)
+            nc.vector.tensor_copy(out=g_parts[:, :, 8 : 8 + n], in_=r2[:, :, 0:n])
 
         def turn_gate():
-            bank = psum.tile([P, 8, P], BF16, name="tp", tag="tp", bufs=2)
+            bank = psum.tile([P, 8, P], BF16, name="tp", tag="tp", bufs=3)
             for i in range(8):
                 nc.tensor.transpose(bank[:, i, :], g_parts[:, i, :], ident_bf[:])
             nc.scalar.copy(out=g_t[:], in_=bank[:])
 
-        def negate_bias(e):
+        def spread_bias(e):
+            bank = psum.tile([P, 512], F32, name="pp", tag="pp", bufs=2)
+            nc.tensor.matmul(out=bank[:], lhsT=ident_bf[:, e : e + 1].to_broadcast([P, P]), rhs=b_rows[:], start=True, stop=True)
             nb[e] = keep.tile([P, F], BF16, name="nb%d" % e, align_bytes=64)
-            nc.vector.tensor_scalar(out=nb[e][:], in0=b_bc[e][:], scalar1=-1.0, scalar2=None, op0=ALU.mult)
+            nc.scalar.activation(out=nb[e][:], in_=bank[:], func=ACT.Copy, scale=-1.0)
 
         LEAD, PLEAD = 3, 2
-        ctx.enter_context(tc.manual_schedule(engines={mybir.EngineType.PE}))
+
         spread_at = {}
         back_at = {5: [0, 1], 6: [2, 3], 7: [4, 5], 8: [6, 7]}
-        hot = psum.tile([P, 512], F32, name="ag", tag="ag", bufs=4)
+        hot = psum.tile([P, 512], F32, name="ag", tag="ag", bufs=3)
 
         def warm(n):
             for i in range(n):
@@ -350,25 +368,31 @@ def tile_relationalgraphmixtureofexperts_x2_kernel(tc, x, a, w, c, b, wg, w0_wor
         nc.scalar.activation(out=zs[:, 0, :], in_=zeros[:, 0:E], func=ACT.Exp)
         warm(6)
         turn_x(0)
-        warm(3)
+        warm(0)
         turn_x(1, True)
-        warm(2)
+        warm(3)
         group_w(0)
         nc.vector.tensor_copy(out=c_f[:], in_=c_bf[:].rearrange("p h t -> p (h t)"))
         quant_w(0)
         quant_x(0)
         turn_x_copy(1, 1, nc.vector.tensor_copy)
-        HP = {0: ("pp", 2), 1: ("pp", 2), 2: ("ag", 4), 3: ("ag", 4), 4: ("ag", 4), 5: ("pp", 2), 6: ("pp", 2), 7: ("ag", 4)}
+        zps = psum.tile([P, 512], F32, name="ag", tag="ag", bufs=3)
+        gate_logits(zps, 0)
+        z = zps[:, 0:32].rearrange("p (i e) -> p i e", e=E)
+        gate_logits(zps, 1)
+        HP = {0: ("pp", 2), 1: ("pp", 2), 2: ("ag", 3), 3: ("ag", 3), 4: ("ag", 3), 5: ("pp", 2), 6: ("pp", 2), 7: ("ag", 3)}
         for i in range(4):
             project(0, i, *HP[i])
         scale_p(0, 0)
         scale_p(0, 2)
+        group_w(1)
         quant_x(1)
+        quant_w(1)
         scale_p(0, 1, True)
         scale_p(0, 3, True)
         turn_a(0, 0)
-        group_p_part(0, 0, 256, F, nc.scalar.copy)
-        group_p_part(0, 0, 0, 256, nc.vector.tensor_copy)
+        group_p_part(0, 0, 320, F, nc.scalar.copy)
+        group_p_part(0, 0, 0, 320, nc.vector.tensor_copy)
         turn_a(0, 1)
         for i in range(4, 8):
             project(0, i, *HP[i])
@@ -378,24 +402,16 @@ def tile_relationalgraphmixtureofexperts_x2_kernel(tc, x, a, w, c, b, wg, w0_wor
         scale_p(0, 7, True)
         quant_p(0, 0)
         turn_a(1, 0)
-        group_p_part(0, 1, 256, F, nc.scalar.copy)
-        group_p_part(0, 1, 0, 256, nc.vector.tensor_copy)
+        group_p_part(0, 1, 320, F, nc.scalar.copy)
+        group_p_part(0, 1, 0, 320, nc.vector.tensor_copy)
         turn_a(1, 1)
         quant_p(0, 1)
         quant_a(0, 0)
         quant_a(0, 1)
-        zps = psum.tile([P, 512], F32, name="ag", tag="ag", bufs=4)
-        gate_logits(zps, 0)
-        gate_logits(zps, 1)
-        z = zps[:, 0:32].rearrange("p (i e) -> p i e", e=E)
-        turn_a(2, 0)
-        turn_a(2, 1)
-        negate_bias(0)
+        spread_bias(0)
         nc.vector.reduce_max(out=zmax[:], in_=z, axis=AX.X)
-        group_w(1)
         nc.vector.tensor_tensor(out=zs[:], in0=z, in1=zmax[:].unsqueeze(2).to_broadcast([P, 8, E]), op=ALU.subtract)
         nc.scalar.activation(out=ez[:], in_=zs[:], func=ACT.Exp)
-        quant_w(1)
         nc.vector.reduce_sum(out=zsum[:], in_=ez[:], axis=AX.X)
 
         def epilogue_1(u, q):
@@ -417,7 +433,8 @@ def tile_relationalgraphmixtureofexperts_x2_kernel(tc, x, a, w, c, b, wg, w0_wor
             share = VC if gp > 0 else 320
             if group and share < F:
                 group_p_part(gp, gh, share, F, nc.scalar.copy)
-            for piece in "ATP":
+            plain = s >= 1 and FORM[pe] == "n"
+            for piece in "aPtbu":
                 if piece == "A" and 0 <= s < STEPS:
                     aggregate(v, q0)
                     aggregate(v, q1)
@@ -425,6 +442,9 @@ def tile_relationalgraphmixtureofexperts_x2_kernel(tc, x, a, w, c, b, wg, w0_wor
                     aggregate(v, q0)
                 if piece == "b" and 0 <= s < STEPS:
                     aggregate(v, q1)
+                if s == 0 and piece in "Tt":
+                    turn_a(2, 0)
+                    turn_a(2, 1)
                 if piece == "T" and turns:
                     turn_a(turn, 0)
                     turn_a(turn, 1)
@@ -440,20 +460,35 @@ def tile_relationalgraphmixtureofexperts_x2_kernel(tc, x, a, w, c, b, wg, w0_wor
                 if piece == "B":
                     for i in back_at.get(s, []):
                         turn_back(i)
-            if "B" not in "ATP":
+            if "B" not in "aPtbu":
                 for i in back_at.get(s, []):
                     turn_back(i)
             for ee, g in spread_at.get(s, []):
                 spread_gate(ee, g)
-            if s == 3 and TURNED:
+            if s == 9:
                 bias_columns()
             if s == 4:
                 turn_gate()
-            if s >= 1:
+            if 12 <= s < STEPS:
+                relu_turned(v, q0)
+                relu_turned(v, q1)
+            if s == 14 or s == STEPS:
+                u = v - 1
+                for t in range(4):
+                    turn_node_tile(u, t, range(4), *(("tp", 3) if t % 2 == 0 else ("pp", 2)))
+                for t in range(4):
+                    weigh_turned(u, t)
+                    store(4 * (u % 2) + t)
+                round_out(u % 2, 0, True)
+                round_out(u % 2, 1, False)
+                quant_out(u % 2, 0)
+                quant_out(u % 2, 1)
+                store_planes(u % 2)
+            if s >= 1 and FORM[pe] != "r":
                 epilogue_1(pv, pq0)
             if group and share > 0:
                 group_p_part(gp, gh, 0, share, nc.vector.tensor_copy)
-            if s >= 1:
+            if s >= 1 and FORM[pe] != "r":
                 epilogue_1(pv, pq1)
             if s == 0:
                 nc.vector.reciprocal(out=zrec[:], in_=zsum[:])
@@ -482,20 +517,6 @@ def tile_relationalgraphmixtureofexperts_x2_kernel(tc, x, a, w, c, b, wg, w0_wor
                 split_gate()
             if s == 3:
                 for ee in PLAIN[1:]:
-                    negate_bias(ee)
+                    spread_bias(ee)
             for i in back_at.get(s, []):
                 add_turned(i)
-            if pe == E - 1 and s >= 1:
-                store(4 * (pv % 2) + pq0)
-                store(4 * (pv % 2) + pq1)
-            if s == STEPS - 1:
-                round_out(0, 0, True)
-                round_out(0, 1, False)
-                quant_out(0, 0)
-                quant_out(0, 1)
-                store_planes(0)
-            if s == STEPS:
-                round_out(1, 1, True)
-                quant_out(1, 1)
-                quant_out(1, 0)
-                store_planes(1)

@@ -21,7 +21,7 @@ FORM = "nnnr"
 TURNED = [e for e in range(E) if FORM[e] == "a"]
 PLAIN = [e for e in range(E) if FORM[e] == "n"]
 LAST = E - 1
-VC = 64
+VC = 0
 
 
 def tile_relationalgraphmixtureofexperts_x2_kernel(tc, x, a, w, c, b, wg, w0_words, w0_scales, out_0, out_1, out_2):
@@ -32,8 +32,6 @@ def tile_relationalgraphmixtureofexperts_x2_kernel(tc, x, a, w, c, b, wg, w0_wor
         psum = ctx.enter_context(tc.psum_pool(name="psum", bufs=2))
 
 
-        zeros = keep.tile([P, F], BF16, name="zeros", align_bytes=64)
-        nc.vector.memset(zeros[:], 0.0)
         ident = keep.tile([P, P], F32, name="ident", align_bytes=64)
         make_identity(nc, ident[:])
         b_rows = keep.tile([P, F], BF16, name="b_rows", align_bytes=64)
@@ -65,15 +63,15 @@ def tile_relationalgraphmixtureofexperts_x2_kernel(tc, x, a, w, c, b, wg, w0_wor
             a_raw[s] = work.tile([P, 2, N], BF16, name="a_raw", tag="raw", bufs=12, align_bytes=64)
             nc.sync.dma_start(out=a_raw[s][:], in_=src[:, 2 * h : 2 * h + 2, :])
 
-        nc.scalar.dma_start(out=c_bf[:], in_=c.rearrange("(h p t) -> p h t", p=P, t=4))
-        nc.scalar.dma_start(out=wg_sb[:], in_=wg.rearrange("(p t) e -> p t e", t=4))
-        for j in range(3):
-            nc.scalar.dma_start(out=b_rows[4 * j : 4 * j + 4, :], in_=b)
         load_x(0)
         load_w(0)
+        nc.sync.dma_start(out=c_bf[:], in_=c.rearrange("(h p t) -> p h t", p=P, t=4))
         load_x(1)
         load_w(1)
+        nc.sync.dma_start(out=wg_sb[:], in_=wg.rearrange("(p t) e -> p t e", t=4))
         load_a(0)
+        for j in range(3):
+            nc.sync.dma_start(out=b_rows[4 * j : 4 * j + 4, :], in_=b)
         load_a(1)
         nc.sync.dma_start(out=w0_codes[:].bitcast(I32), in_=w0_words[0].rearrange("p n t -> p (n t)").bitcast(I32))
         for q in range(4):
@@ -337,11 +335,11 @@ def tile_relationalgraphmixtureofexperts_x2_kernel(tc, x, a, w, c, b, wg, w0_wor
 
         def split_gate():
             n = len(PLAIN) + len(TURNED)
-            nc.vector.tensor_copy(out=g_parts[:, :, 0:n], in_=gate[:, :, 0:n])
-            nc.vector.tensor_tensor(out=r1[:, :, 0:n], in0=gate[:, :, 0:n], in1=g_parts[:, :, 0:n], op=ALU.subtract)
-            nc.vector.tensor_copy(out=g_parts[:, :, 4 : 4 + n], in_=r1[:, :, 0:n])
-            nc.vector.tensor_tensor(out=r2[:, :, 0:n], in0=r1[:, :, 0:n], in1=g_parts[:, :, 4 : 4 + n], op=ALU.subtract)
-            nc.vector.tensor_copy(out=g_parts[:, :, 8 : 8 + n], in_=r2[:, :, 0:n])
+            nc.gpsimd.tensor_copy(out=g_parts[:, :, 0:n], in_=gate[:, :, 0:n])
+            nc.gpsimd.tensor_tensor(out=r1[:, :, 0:n], in0=gate[:, :, 0:n], in1=g_parts[:, :, 0:n], op=ALU.subtract)
+            nc.gpsimd.tensor_copy(out=g_parts[:, :, 4 : 4 + n], in_=r1[:, :, 0:n])
+            nc.gpsimd.tensor_tensor(out=r2[:, :, 0:n], in0=r1[:, :, 0:n], in1=g_parts[:, :, 4 : 4 + n], op=ALU.subtract)
+            nc.gpsimd.tensor_copy(out=g_parts[:, :, 8 : 8 + n], in_=r2[:, :, 0:n])
 
         def turn_gate():
             bank = psum.tile([P, 8, P], BF16, name="tp", tag="tp", bufs=3)
@@ -359,18 +357,8 @@ def tile_relationalgraphmixtureofexperts_x2_kernel(tc, x, a, w, c, b, wg, w0_wor
 
         spread_at = {}
         back_at = {5: [0, 1], 6: [2, 3], 7: [4, 5], 8: [6, 7]}
-        hot = psum.tile([P, 512], F32, name="ag", tag="ag", bufs=3)
-
-        def warm(n):
-            for i in range(n):
-                nc.tensor.matmul(out=hot[:], lhsT=zeros[:, 0:P], rhs=zeros[:], start=True, stop=True)
-
-        nc.scalar.activation(out=zs[:, 0, :], in_=zeros[:, 0:E], func=ACT.Exp)
-        warm(6)
         turn_x(0)
-        warm(0)
         turn_x(1, True)
-        warm(3)
         group_w(0)
         nc.vector.tensor_copy(out=c_f[:], in_=c_bf[:].rearrange("p h t -> p (h t)"))
         quant_w(0)
@@ -434,7 +422,7 @@ def tile_relationalgraphmixtureofexperts_x2_kernel(tc, x, a, w, c, b, wg, w0_wor
             if group and share < F:
                 group_p_part(gp, gh, share, F, nc.scalar.copy)
             plain = s >= 1 and FORM[pe] == "n"
-            for piece in "aPtbu":
+            for piece in "APT":
                 if piece == "A" and 0 <= s < STEPS:
                     aggregate(v, q0)
                     aggregate(v, q1)
@@ -460,7 +448,7 @@ def tile_relationalgraphmixtureofexperts_x2_kernel(tc, x, a, w, c, b, wg, w0_wor
                 if piece == "B":
                     for i in back_at.get(s, []):
                         turn_back(i)
-            if "B" not in "aPtbu":
+            if "B" not in "APT":
                 for i in back_at.get(s, []):
                     turn_back(i)
             for ee, g in spread_at.get(s, []):

from contextlib import ExitStack

import concourse.mybir as mybir
from concourse.masks import make_identity

F32 = mybir.dt.float32
BF16 = mybir.dt.bfloat16
U32 = mybir.dt.uint32
I32 = mybir.dt.int32
U8 = mybir.dt.uint8
FP8X4 = mybir.dt.float8_e4m3fn_x4
ACT = mybir.ActivationFunctionType
ALU = mybir.AluOpType
AX = mybir.AxisListType

N, D, F, E = 1024, 512, 512, 4
P = 128
FLOPS = 2 * (E * N * D * F + E * N * N * F + N * D * F)
STEPS = 16
FORM = "nnnr"
TURNED = [e for e in range(E) if FORM[e] == "a"]
PLAIN = [e for e in range(E) if FORM[e] == "n"]
LAST = E - 1
VC = 0


def tile_relationalgraphmixtureofexperts_x2_kernel(tc, x, a, w, c, b, wg, w0_words, w0_scales, out_0, out_1, out_2):
    nc = tc.nc
    with ExitStack() as ctx:
        keep = ctx.enter_context(tc.tile_pool(name="keep", bufs=1))
        work = ctx.enter_context(tc.tile_pool(name="work", bufs=3))
        psum = ctx.enter_context(tc.psum_pool(name="psum", bufs=2))


        ident = keep.tile([P, P], F32, name="ident", align_bytes=64)
        make_identity(nc, ident[:])
        b_rows = keep.tile([P, F], BF16, name="b_rows", align_bytes=64)
        nc.gpsimd.memset(b_rows[:], 0.0)
        w0_sc = keep.tile([P, F], U8, name="w0_sc", align_bytes=64)
        nc.gpsimd.memset(w0_sc[:].bitcast(I32), 0)
        ident_bf = keep.tile([P, P], BF16, name="ident_bf", align_bytes=64)
        make_identity(nc, ident_bf[:])
        g_parts = keep.tile([P, 8, P], BF16, name="g_parts", align_bytes=64)
        nc.gpsimd.memset(g_parts[:], 0.0)

        w0_codes = keep.tile([P, 4 * F], U8, name="w0_codes", align_bytes=64)
        c_bf = keep.tile([P, 2, 4], BF16, name="c_bf", align_bytes=64)
        wg_sb = keep.tile([P, 4, E], BF16, name="wg_sb", align_bytes=64)
        x_raw, w_raw, a_raw = {}, {}, {}
        nb = {}

        def load_x(g):
            x_raw[g] = work.tile([P, 4, D], BF16, name="x_raw", tag="raw", bufs=12, align_bytes=64)
            nc.sync.dma_start(out=x_raw[g][:], in_=x[512 * g : 512 * g + 512, :].rearrange("(p t) k -> p t k", t=4))

        def load_w(e):
            w_raw[e] = work.tile([P, 4, F], BF16, name="w_raw", tag="raw", bufs=12, align_bytes=64)
            nc.sync.dma_start(out=w_raw[e][:], in_=w[e].rearrange("(p j) f -> p j f", j=4))

        def load_a(s):
            e, g, h = s // 4, (s // 2) % 2, s % 2
            src = a[e, 512 * g : 512 * g + 512, :].rearrange("(p t) m -> p t m", t=4)
            a_raw[s] = work.tile([P, 2, N], BF16, name="a_raw", tag="raw", bufs=12, align_bytes=64)
            nc.sync.dma_start(out=a_raw[s][:], in_=src[:, 2 * h : 2 * h + 2, :])

        load_x(0)
        load_w(0)
        nc.sync.dma_start(out=c_bf[:], in_=c.rearrange("(h p t) -> p h t", p=P, t=4))
        load_x(1)
        load_w(1)
        nc.sync.dma_start(out=wg_sb[:], in_=wg.rearrange("(p t) e -> p t e", t=4))
        load_a(0)
        for j in range(3):
            nc.sync.dma_start(out=b_rows[4 * j : 4 * j + 4, :], in_=b)
        load_a(1)
        nc.sync.dma_start(out=w0_codes[:].bitcast(I32), in_=w0_words[0].rearrange("p n t -> p (n t)").bitcast(I32))
        for q in range(4):
            nc.sync.dma_start(out=w0_sc[32 * q : 32 * q + 4, :].bitcast(I32), in_=w0_scales[0, 4 * q : 4 * q + 4, :].bitcast(I32))
        load_a(2)
        load_a(3)
        load_w(2)
        for s in range(4, 8):
            load_a(s)
        load_w(3)
        for s in range(8, STEPS):
            load_a(s)

        x_t = work.tile([P, 4096], BF16, name="x_t", tag="a_t", bufs=3, align_bytes=64)
        x_codes = keep.tile([P, 8 * P], U32, name="x_codes", align_bytes=64)
        x_sc = keep.tile([P, 8 * P], U8, name="x_sc", align_bytes=64)

        x_bank = {}

        def turn_x(g, hold=False):
            words = x_raw[g][:].rearrange("p t k -> p (t k)").bitcast(F32)
            for half in range(2):
                bank = psum.tile([P, 512], F32, name="tp", tag="tp", bufs=3)
                x_bank[g, half] = bank
                for tt in range(2):
                    for u in range(2):
                        lo = 256 * (2 * half + tt) + u
                        nc.tensor.transpose(bank[:, 128 * (2 * tt + u) : 128 * (2 * tt + u) + 128], words[:, lo : lo + 256 - u : 2], ident[:])
                if half == 0 or not hold:
                    turn_x_copy(g, half, nc.scalar.copy)

        def turn_x_copy(g, half, copy):
            c0 = 2048 * g + 1024 * half
            copy(
                out=x_t[:, c0 : c0 + 1024].bitcast(F32).rearrange("p (t n u) -> p t n u", t=2, u=2),
                in_=x_bank[g, half][:].rearrange("p (t u n) -> p t n u", t=2, u=2),
            )

        def quant_x(g):
            cols = slice(512 * g, 512 * g + 512)
            nc.vector.quantize_mx(out=x_codes[:, cols].bitcast(FP8X4), scales=x_sc[:, cols], in_=x_t[:, 2048 * g : 2048 * g + 2048])

        w_codes, w_sc, w_grp = {}, {}, {}

        def group_w(e):
            w_grp[e] = work.tile([P, F, 4], BF16, name="w_grp", tag="grp", bufs=5, align_bytes=64)
            nc.vector.tensor_copy(out=w_grp[e][:].rearrange("p (f i) j -> p f j i", i=4), in_=w_raw[e][:].rearrange("p j (f i) -> p f j i", i=4))

        def quant_w(e):
            w_codes[e] = keep.tile([P, F], U32, name="w_codes%d" % e, align_bytes=64)
            w_sc[e] = keep.tile([P, F], U8, name="w_sc%d" % e, align_bytes=64)
            nc.vector.quantize_mx(out=w_codes[e][:].bitcast(FP8X4), scales=w_sc[e][:], in_=w_grp[e][:].rearrange("p f j -> p (f j)"))

        a_t, a_codes, a_sc = {}, {}, {}

        def turn_a(s, tt):
            v, half = s // 2, s % 2
            words = a_raw[s][:].rearrange("p t m -> p (t m)").bitcast(F32)
            if half == 0 and tt == 0:
                a_t[v] = work.tile([P, 4096], BF16, name="a_t", tag="a_t", bufs=3, align_bytes=64)
            dst = a_t[v][:].bitcast(F32).rearrange("p (h t n u) -> p h t n u", h=2, t=4, u=2)
            bank = psum.tile([P, 512], F32, name="tp", tag="tp", bufs=3)
            for h in range(2):
                for u in range(2):
                    lo = 512 * tt + 256 * h + u
                    nc.tensor.transpose(bank[:, 128 * (2 * h + u) : 128 * (2 * h + u) + 128], words[:, lo : lo + 256 - u : 2], ident[:])
            nc.scalar.copy(out=dst[:, :, 2 * half + tt], in_=bank[:].rearrange("p (h u n) -> p h n u", h=2, u=2))

        def quant_a(v, h):
            if h == 0:
                a_codes[v] = work.tile([P, 1024], U32, name="a_codes", tag="a_codes", bufs=3, align_bytes=64)
                a_sc[v] = work.tile([P, 1024], U8, name="a_sc", tag="a_sc", bufs=3, align_bytes=64)
            cols = slice(512 * h, 512 * h + 512)
            nc.vector.quantize_mx(out=a_codes[v][:, cols].bitcast(FP8X4), scales=a_sc[v][:, cols], in_=a_t[v][:, 2048 * h : 2048 * h + 2048])

        p_raw, p_grp, p_codes, p_sc = {}, {}, {}, {}

        def mx(out, lhs, rhs, start, stop):
            nc.tensor.matmul_mx(
                out=out, lhsT=lhs[0].bitcast(FP8X4), lhsT_scale=lhs[1], rhs=rhs[0].bitcast(FP8X4), rhs_scale=rhs[1], start=start, stop=stop
            )

        def x_tile(i):
            return x_codes[:, 128 * i : 128 * i + 128], x_sc[:, 128 * i : 128 * i + 128]

        banks = {}

        def project(e, i, tag="pp", bufs=2):
            banks[e, i] = psum.tile([P, 512], F32, name=tag, tag=tag, bufs=bufs)
            mx(banks[e, i][:], x_tile(i), (w_codes[e][:], w_sc[e][:]), True, True)

        def scale_p(e, i, on_vector=False):
            h, t = i // 4, i % 4
            if t == 0:
                p_raw[e, h] = work.tile([P, 4, F], BF16, name="p_raw", tag="p_raw", bufs=3, align_bytes=64)
            dst = p_raw[e, h][:, t, :]
            if on_vector:
                nc.vector.tensor_scalar(out=dst, in0=banks[e, i][:], scalar1=c_f[:, i : i + 1], scalar2=None, op0=ALU.mult)
            else:
                nc.scalar.activation(out=dst, in_=banks[e, i][:], func=ACT.Copy, scale=c_f[:, i : i + 1])

        def group_p(e, h, vc=VC):
            if vc > 0:
                group_p_part(e, h, 0, vc, nc.vector.tensor_copy)
            if vc < F:
                group_p_part(e, h, vc, F, nc.scalar.copy)

        def group_p_part(e, h, f0, f1, copy):
            if (e, h) not in p_grp:
                p_grp[e, h] = work.tile([P, F, 4], BF16, name="p_grp", tag="grp", bufs=5, align_bytes=64)
            dst = p_grp[e, h][:].rearrange("p (f i) t -> p f t i", i=4)
            src = p_raw[e, h][:].rearrange("p t (f i) -> p f t i", i=4)
            copy(out=dst[:, f0 // 4 : f1 // 4], in_=src[:, f0 // 4 : f1 // 4])

        def quant_p(e, h):
            p_codes[e, h] = work.tile([P, F], U32, name="p_codes", tag="p_codes", bufs=5, align_bytes=64)
            p_sc[e, h] = work.tile([P, F], U8, name="p_sc", tag="p_sc", bufs=5, align_bytes=64)
            nc.vector.quantize_mx(out=p_codes[e, h][:].bitcast(FP8X4), scales=p_sc[e, h][:], in_=p_grp[e, h][:].rearrange("p f t -> p (f t)"))

        agg, proj0 = {}, {}

        def aggregate(v, q):
            e, g = v // 2, v % 2
            agg[v, q] = psum.tile([P, 512], F32, name="ag", tag="ag", bufs=3)
            for h in range(2):
                if FORM[e] != "n":
                    fs = slice(128 * q, 128 * q + 128)
                    lhs = (p_codes[e, h][:, fs], p_sc[e, h][:, fs])
                    rhs = (a_codes[v][:, 512 * h : 512 * h + 512], a_sc[v][:, 512 * h : 512 * h + 512])
                else:
                    ns = slice(512 * h + 128 * q, 512 * h + 128 * q + 128)
                    lhs = (a_codes[v][:, ns], a_sc[v][:, ns])
                    rhs = (p_codes[e, h][:], p_sc[e, h][:])
                mx(agg[v, q][:], lhs, rhs, h == 0, h == 1)
            if e == PLAIN[0]:
                proj0[v, q] = psum.tile([P, 512], F32, name="ag", tag="ag", bufs=3)
                mx(proj0[v, q][:], x_tile(4 * g + q), (w0_codes[:], w0_sc[:]), True, True)

        acc = keep.tile([P, 8, F], F32, name="acc", align_bytes=64)
        u_t, turned, res, sums = {}, {}, {}, {}

        def clamp(v, q):
            u_t[v, q] = work.tile([P, F], F32, name="u_t", tag="u_t", bufs=4, align_bytes=64)
            nc.vector.tensor_tensor(out=u_t[v, q][:], in0=agg[v, q][:], in1=nb[v // 2][:], op=ALU.max)

        def relu_turned(v, q):
            if q == 0:
                turned[v] = work.tile([P, 4, F], F32, name="turned", tag="big", bufs=4, align_bytes=64)
            nc.scalar.activation(out=turned[v][:, q, :], in_=agg[v, q][:], func=ACT.Relu, bias=nb_col[:, q, LAST : LAST + 1])

        def turn_node_tile(v, t, qs, tag, bufs):
            i = 4 * (v % 2) + t
            if 0 in qs:
                sums[i] = psum.tile([P, 512], F32, name=tag, tag=tag, bufs=bufs)
            for q in qs:
                nc.tensor.transpose(sums[i][:, 128 * q : 128 * q + 128], turned[v][:, q, 128 * t : 128 * t + 128], ident[:])

        def weigh_turned(v, t):
            i = 4 * (v % 2) + t
            nc.vector.scalar_tensor_tensor(
                out=result(i), in0=sums[i][:], scalar=gate[:, i, LAST : LAST + 1], in1=acc[:, i, :], op0=ALU.mult, op1=ALU.add
            )

        def result(i):
            if i % 4 == 0 and i // 4 not in res:
                res[i // 4] = work.tile([P, 4, F], F32, name="res", tag="big", bufs=4, align_bytes=64)
            return res[i // 4][:, i % 4, :]

        def weigh(v, q, f0=0, f1=F):
            e, i = v // 2, 4 * (v % 2) + q
            other = proj0[v, q][:] if e == PLAIN[0] else acc[:, i, :]
            dst = result(i) if e == E - 1 else acc[:, i, :]
            nc.vector.scalar_tensor_tensor(
                out=dst[:, f0:f1], in0=u_t[v, q][:, f0:f1], scalar=gate[:, i, e : e + 1], in1=other[:, f0:f1], op0=ALU.mult, op1=ALU.add
            )

        def clamp_weigh(v, q):
            e, g = v // 2, v % 2
            if q == 0:
                turned[v] = work.tile([P, 4, F], F32, name="turned", tag="big", bufs=4, align_bytes=64)
            nc.vector.scalar_tensor_tensor(
                out=turned[v][:, q, :], in0=agg[v, q][:], scalar=nb_col[:, q, e : e + 1], in1=g_rows[e][:, 512 * g : 512 * g + 512], op0=ALU.max, op1=ALU.mult
            )

        def turn_back(i, tag="ag", bufs=3):
            g, t = i // 4, i % 4
            sums[i] = psum.tile([P, 512], F32, name=tag, tag=tag, bufs=bufs)
            nc.tensor.matmul(out=sums[i][:], lhsT=g_t[:, i, :], rhs=b_rows[:], start=True, stop=not TURNED)
            for e in TURNED:
                for q in range(4):
                    nc.tensor.matmul(
                        out=sums[i][:, 128 * q : 128 * q + 128],
                        lhsT=turned[2 * e + g][:, q, 128 * t : 128 * t + 128],
                        rhs=ident[:],
                        is_transpose=True,
                        start=False,
                        stop=(e == TURNED[-1] and q == 3),
                    )

        def add_turned(i):
            dst = acc[:, i, :]
            nc.vector.tensor_tensor(out=dst, in0=sums[i][:], in1=acc[:, i, :], op=ALU.add)

        def store(i):
            g, t = i // 4, i % 4
            nc.sync.dma_start(out=out_0[512 * g : 512 * g + 512, :].rearrange("(p t) m -> p t m", t=4)[:, t, :], in_=res[g][:, t, :])

        o_grp, o_codes, o_sc = {}, {}, {}

        def round_out(g, part, on_vector):
            if g not in o_grp:
                o_grp[g] = work.tile([P, F, 4], BF16, name="o_grp", tag="grp", bufs=5, align_bytes=64)
                o_codes[g] = work.tile([P, F], U32, name="o_codes", tag="p_codes", bufs=5, align_bytes=64)
                o_sc[g] = work.tile([P, F], U8, name="o_sc", tag="p_sc", bufs=5, align_bytes=64)
            f0 = 256 * part
            dst = o_grp[g][:, f0 : f0 + 256, :].rearrange("p (f i) t -> p f t i", i=4)
            src = res[g][:, :, f0 : f0 + 256].rearrange("p t (f i) -> p f t i", i=4)
            if on_vector:
                nc.vector.tensor_copy(out=dst, in_=src)
            else:
                nc.scalar.copy(out=dst, in_=src)

        def quant_out(g, part):
            cols = slice(256 * part, 256 * part + 256)
            nc.vector.quantize_mx(out=o_codes[g][:, cols].bitcast(FP8X4), scales=o_sc[g][:, cols], in_=o_grp[g][:, cols, :].rearrange("p f t -> p (f t)"))

        def store_planes(g):
            nc.sync.dma_start(out=out_1[g].rearrange("p m t -> p (m t)").bitcast(I32), in_=o_codes[g][:].bitcast(I32))
            for q in range(4):
                nc.sync.dma_start(out=out_2[g, 4 * q : 4 * q + 4, :].bitcast(I32), in_=o_sc[g][32 * q : 32 * q + 4, :].bitcast(I32))

        def small(name, shape):
            return keep.tile(shape, F32, name=name, align_bytes=64)

        c_f = small("c_f", [P, 8])
        nb_col = small("nb_col", [P, 4, E])
        zmax, zsum, zrec = small("zmax", [P, 8]), small("zsum", [P, 8]), small("zrec", [P, 8])
        zs, ez, gate = small("zs", [P, 8, E]), small("ez", [P, 8, E]), small("gate", [P, 8, E])
        r1, r2 = small("r1", [P, 8, E]), small("r2", [P, 8, E])
        g_rows = {e: small("g_rows%d" % e, [P, N]) for e in TURNED}
        g_t = keep.tile([P, 8, P], BF16, name="g_t", align_bytes=64)

        def gate_logits(zps, g):
            for i in range(4 * g, 4 * g + 4):
                xs = x_t[:, 512 * i : 512 * i + 512].rearrange("p (n j) -> p n j", j=4)
                for j in range(4):
                    nc.tensor.matmul(out=zps[:, 4 * i : 4 * i + 4], lhsT=xs[:, :, j], rhs=wg_sb[:, j, :], start=(j == 0), stop=(j == 3))

        def bias_columns():
            bank = psum.tile([P, 4, P], BF16, name="tp", tag="tp", bufs=3)
            for q in range(4):
                nc.tensor.transpose(bank[:, q, :], b_rows[:, 128 * q : 128 * q + 128], ident_bf[:])
            nc.scalar.activation(out=nb_col[:, :, 0:LAST], in_=bank[:, :, 0:LAST], func=ACT.Copy, scale=-1.0)
            nc.scalar.activation(out=nb_col[:, :, LAST:E], in_=bank[:, :, LAST:E], func=ACT.Copy)

        def spread_gate(e, g):
            bank = psum.tile([P, 512], F32, name="tp", tag="tp", bufs=3)
            for t in range(4):
                nc.tensor.transpose(bank[:, 128 * t : 128 * t + 128], gate[:, 4 * g + t, e : e + 1].to_broadcast([P, P]), ident[:])
            nc.scalar.copy(out=g_rows[e][:, 512 * g : 512 * g + 512], in_=bank[:])

        def split_gate():
            n = len(PLAIN) + len(TURNED)
            nc.gpsimd.tensor_copy(out=g_parts[:, :, 0:n], in_=gate[:, :, 0:n])
            nc.gpsimd.tensor_tensor(out=r1[:, :, 0:n], in0=gate[:, :, 0:n], in1=g_parts[:, :, 0:n], op=ALU.subtract)
            nc.gpsimd.tensor_copy(out=g_parts[:, :, 4 : 4 + n], in_=r1[:, :, 0:n])
            nc.gpsimd.tensor_tensor(out=r2[:, :, 0:n], in0=r1[:, :, 0:n], in1=g_parts[:, :, 4 : 4 + n], op=ALU.subtract)
            nc.gpsimd.tensor_copy(out=g_parts[:, :, 8 : 8 + n], in_=r2[:, :, 0:n])

        def turn_gate():
            bank = psum.tile([P, 8, P], BF16, name="tp", tag="tp", bufs=3)
            for i in range(8):
                nc.tensor.transpose(bank[:, i, :], g_parts[:, i, :], ident_bf[:])
            nc.scalar.copy(out=g_t[:], in_=bank[:])

        def spread_bias(e):
            bank = psum.tile([P, 512], F32, name="pp", tag="pp", bufs=2)
            nc.tensor.matmul(out=bank[:], lhsT=ident_bf[:, e : e + 1].to_broadcast([P, P]), rhs=b_rows[:], start=True, stop=True)
            nb[e] = keep.tile([P, F], BF16, name="nb%d" % e, align_bytes=64)
            nc.scalar.activation(out=nb[e][:], in_=bank[:], func=ACT.Copy, scale=-1.0)

        LEAD, PLEAD = 3, 2

        spread_at = {}
        back_at = {5: [0, 1], 6: [2, 3], 7: [4, 5], 8: [6, 7]}
        turn_x(0)
        turn_x(1, True)
        group_w(0)
        nc.vector.tensor_copy(out=c_f[:], in_=c_bf[:].rearrange("p h t -> p (h t)"))
        quant_w(0)
        quant_x(0)
        turn_x_copy(1, 1, nc.vector.tensor_copy)
        zps = psum.tile([P, 512], F32, name="ag", tag="ag", bufs=3)
        gate_logits(zps, 0)
        z = zps[:, 0:32].rearrange("p (i e) -> p i e", e=E)
        gate_logits(zps, 1)
        HP = {0: ("pp", 2), 1: ("pp", 2), 2: ("ag", 3), 3: ("ag", 3), 4: ("ag", 3), 5: ("pp", 2), 6: ("pp", 2), 7: ("ag", 3)}
        for i in range(4):
            project(0, i, *HP[i])
        scale_p(0, 0)
        scale_p(0, 2)
        group_w(1)
        quant_x(1)
        quant_w(1)
        scale_p(0, 1, True)
        scale_p(0, 3, True)
        turn_a(0, 0)
        group_p_part(0, 0, 320, F, nc.scalar.copy)
        group_p_part(0, 0, 0, 320, nc.vector.tensor_copy)
        turn_a(0, 1)
        for i in range(4, 8):
            project(0, i, *HP[i])
        scale_p(0, 4)
        scale_p(0, 5, True)
        scale_p(0, 6)
        scale_p(0, 7, True)
        quant_p(0, 0)
        turn_a(1, 0)
        group_p_part(0, 1, 320, F, nc.scalar.copy)
        group_p_part(0, 1, 0, 320, nc.vector.tensor_copy)
        turn_a(1, 1)
        quant_p(0, 1)
        quant_a(0, 0)
        quant_a(0, 1)
        spread_bias(0)
        nc.vector.reduce_max(out=zmax[:], in_=z, axis=AX.X)
        nc.vector.tensor_tensor(out=zs[:], in0=z, in1=zmax[:].unsqueeze(2).to_broadcast([P, 8, E]), op=ALU.subtract)
        nc.scalar.activation(out=ez[:], in_=zs[:], func=ACT.Exp)
        nc.vector.reduce_sum(out=zsum[:], in_=ez[:], axis=AX.X)

        def epilogue_1(u, q):
            (clamp if FORM[u // 2] == "n" else clamp_weigh)(u, q)

        for s in range(STEPS + 1):
            v, e, j = s // 2, s // 4, s % 4
            q0, q1 = 2 * (s % 2), 2 * (s % 2) + 1
            pv, pe = (s - 1) // 2, (s - 1) // 4
            pq0, pq1 = 2 * ((s - 1) % 2), 2 * ((s - 1) % 2) + 1
            plain = s >= 1 and FORM[pe] == "n"
            turn = s + LEAD
            turns = 0 <= turn < STEPS
            ne = max(e + 1 if j < 3 else e + 2, 1)
            pairs = {-1: [], 0: [0, 1], 1: [2], 2: [3]}[s] if s < 3 else [(j + 1) % 4]
            gp, gh = e + 1, j // 2
            group = j % 2 == 1 and gp < E and s < STEPS
            quant = j >= 2 and gp < E and s < STEPS
            share = VC if gp > 0 else 320
            if group and share < F:
                group_p_part(gp, gh, share, F, nc.scalar.copy)
            plain = s >= 1 and FORM[pe] == "n"
            for piece in "APT":
                if piece == "A" and 0 <= s < STEPS:
                    aggregate(v, q0)
                    aggregate(v, q1)
                if piece == "a" and 0 <= s < STEPS:
                    aggregate(v, q0)
                if piece == "b" and 0 <= s < STEPS:
                    aggregate(v, q1)
                if s == 0 and piece in "Tt":
                    turn_a(2, 0)
                    turn_a(2, 1)
                if piece == "T" and turns:
                    turn_a(turn, 0)
                    turn_a(turn, 1)
                if piece == "t" and turns:
                    turn_a(turn, 0)
                if piece == "u" and turns:
                    turn_a(turn, 1)
                if piece == "P" and ne < E and s < STEPS:
                    for k in pairs:
                        for i in (2 * k, 2 * k + 1):
                            project(ne, i)
                            scale_p(ne, i)
                if piece == "B":
                    for i in back_at.get(s, []):
                        turn_back(i)
            if "B" not in "APT":
                for i in back_at.get(s, []):
                    turn_back(i)
            for ee, g in spread_at.get(s, []):
                spread_gate(ee, g)
            if s == 9:
                bias_columns()
            if s == 4:
                turn_gate()
            if 12 <= s < STEPS:
                relu_turned(v, q0)
                relu_turned(v, q1)
            if s == 14 or s == STEPS:
                u = v - 1
                for t in range(4):
                    turn_node_tile(u, t, range(4), *(("tp", 3) if t % 2 == 0 else ("pp", 2)))
                for t in range(4):
                    weigh_turned(u, t)
                    store(4 * (u % 2) + t)
                round_out(u % 2, 0, True)
                round_out(u % 2, 1, False)
                quant_out(u % 2, 0)
                quant_out(u % 2, 1)
                store_planes(u % 2)
            if s >= 1 and FORM[pe] != "r":
                epilogue_1(pv, pq0)
            if group and share > 0:
                group_p_part(gp, gh, 0, share, nc.vector.tensor_copy)
            if s >= 1 and FORM[pe] != "r":
                epilogue_1(pv, pq1)
            if s == 0:
                nc.vector.reciprocal(out=zrec[:], in_=zsum[:])
            if s % 2 == 1 and 0 <= (s - 1) // 2 + 1 < 8:
                quant_a((s - 1) // 2 + 1, 0)
            if plain:
                weigh(pv, pq0)
            if s == 0:
                nc.vector.tensor_tensor(out=gate[:], in0=ez[:], in1=zrec[:].unsqueeze(2).to_broadcast([P, 8, E]), op=ALU.mult)
            if s % 2 == 1 and 0 <= (s - 1) // 2 + 1 < 8:
                quant_a((s - 1) // 2 + 1, 1)
            if quant:
                quant_p(gp, j - 2)
            if s == 1 or s == 5:
                group_w(2 if s == 1 else 3)
            if plain:
                if s == STEPS:
                    weigh(pv, pq1, 0, 256)
                    round_out(1, 0, False)
                    weigh(pv, pq1, 256, 512)
                else:
                    weigh(pv, pq1)
            if s == 2 or s == 6:
                quant_w(2 if s == 2 else 3)
            if s == 2:
                split_gate()
            if s == 3:
                for ee in PLAIN[1:]:
                    spread_bias(ee)
            for i in back_at.get(s, []):
                add_turned(i)
